import numpy as np, ml_dtypes
CORES = [40,41,42,43,44,45,46,47]
N = 8
BF = ml_dtypes.bfloat16
def gentries(a):
    return np.ascontiguousarray(a.reshape(8, 16, -1).transpose(0, 2, 1)).reshape(8, -1)
def gtable(e):
    e = np.asarray(e); return np.ascontiguousarray(e.reshape(8, -1, 16).transpose(0, 2, 1)).reshape(128, -1).astype(np.int32)
def f(rng, *shape):
    return (rng.standard_normal(shape, dtype=np.float32) * np.exp2(rng.integers(-2, 3, shape[:-1] + (1,)))).astype(BF)
def wide(rng, *shape):
    v = f(rng, *shape).astype(np.float32); k = shape[:-2] + (1, shape[-1])
    return (v * np.exp2(rng.integers(-6, 7, k)) * (rng.random(k) > 0.0625)).astype(BF)
F, P, KD, GEN, LG, RO = 4096, 1024, 4, 4, 2, 2
S, H = F + 2 * P, F // 2
def pointers(pl, b):
    return np.concatenate([np.broadcast_to(np.arange(F), (N, 8, F)), 2 * pl + b], axis=2)
def rise(q):
    for i in range(LG): q = np.take_along_axis(q, q, 2)
    return q
def alleles(rng):
    u = rng.random((N, 8, 16, F), dtype=np.float32)
    return np.floor(16 * u * np.sqrt(u)) * np.exp2(rng.integers(-2, 3, (N, 8, 16, 1))).astype(np.float32)
def generations(rng):
    e = rng.choice(np.array([0.7, 1.0, 1.4]), (N, 8, 1))
    return np.minimum(1 + (GEN * rng.random((N, 8, P)) ** e).astype(np.int64), GEN)
def pedigree(rng, gl, near):
    pl = np.zeros((N, 8, 2 * P), np.int64)
    for r in range(N):
        for g in range(8):
            k = gl[r, g]; o = np.argsort(k, kind="stable"); ids = np.concatenate([np.arange(H), H + o])
            under = np.searchsorted(k[o], np.arange(GEN + 2)); kk = np.repeat(k, 2)
            top = H + under[kk]; low = np.where(kk == 1, 0, H + under[kk - 1])
            low = np.where((rng.random(2 * P) < near) & (low < top), low, 0)
            pl[r, g] = ids[low + (rng.random(2 * P) * (top - low)).astype(np.int64)]
    return pl
def kids(rng, pl):
    kl = rng.integers(F, S, (N, 8, KD, P))
    for r in range(N):
        for g in range(8):
            v = pl[r, g]; o = np.lexsort((rng.random(2 * P), v)); at = np.searchsorted(v[o], H + np.arange(P + 1))
            for k in range(KD):
                kl[r, g, k] = np.where(at[:-1] + k < at[1:], F + o[np.minimum(at[:-1] + k, 2 * P - 1)], kl[r, g, k])
    return kl
def phenotypes(rng, al, pl, tb):
    a = rise(pointers(pl, tb))[:, :, F:].reshape(N, 8, 1, P, 2)
    y = np.maximum(np.take_along_axis(al, a[..., 0], 3), np.take_along_axis(al, a[..., 1], 3))
    return np.where(rng.random(y.shape) < 0.0625, np.take_along_axis(al, rng.integers(0, F, y.shape), 3), y)
def start(rng, tb):
    return tb ^ (rng.random((1, 8, 2 * P)) < 0.2).astype(np.int64) ^ (rng.random((N, 8, 2 * P)) < 0.1).astype(np.int64)
def pack(al, y, pl, b, kl, gl):
    return {"fa": np.ascontiguousarray(al.reshape(N, 128, F)).astype(BF), "ph": np.ascontiguousarray(y.reshape(N, 128, P)).astype(BF),
            "par": np.stack([gtable(a) for a in pl]), "sw": np.stack([gtable(a) for a in b]),
            "kd": np.stack([gtable(a.reshape(8, -1)) for a in kl]), "gen": np.ascontiguousarray(gl).astype(np.int32)}
def finish(rng, al, gl, pl, kl):
    tb = rng.integers(0, 2, (N, 8, 2 * P)); y = phenotypes(rng, al, pl, tb)
    return pack(al, y, pl, start(rng, tb), kl, gl)
def own():
    return F + 2 * np.arange(P)[None, :] + np.arange(KD)[:, None] % 2
def setup_inputs(rng):
    al = alleles(rng); gl = generations(rng); pl = pedigree(rng, gl, 0.85)
    return finish(rng, al, gl, pl, kids(rng, pl))
def setup_inputs_deep(rng):
    al = alleles(rng); gl = np.tile(GEN - np.arange(P) * GEN // P, (N, 8, 1)); gl[:, 1::2] = rng.permuted(gl[:, 1::2], axis=2)
    pl = pedigree(rng, gl, 1.0); one = np.repeat(gl[:, 0], 2, axis=1) == 1
    pl[:, 0] = np.where(one, rng.choice(np.array([0, H - 1]), one.shape), pl[:, 0])
    return finish(rng, al, gl, pl, kids(rng, pl))
def setup_inputs_full(rng):
    h = H // 2; up = rng.integers(0, 2, (N, 8, H)); v = rng.integers(0, 4, (N, 8, 16, H, 2))
    tall = up[:, :, None, :h, None] == np.arange(2)
    v[:, :, :, :h] = np.where(tall, rng.integers(10, 16, (N, 8, 16, h, 2)), rng.integers(4, 10, (N, 8, 16, h, 2)))
    unit = np.exp2(rng.integers(-2, 3, (N, 8, 16, 1))).astype(np.float32); al = v.reshape(N, 8, 16, F).astype(np.float32) * unit
    e = rng.integers(0, 2, (8, P)); pl = rng.integers(h, H, (N, 8, P, 2)); tb = rng.integers(0, 2, (N, 8, P, 2)); b = tb.copy()
    gl = np.full((N, 8, P), 2); kl = rng.integers(F, S, (N, 8, KD, P)); near = np.zeros((8, P), bool); weak = np.zeros((N, 8, P), bool)
    top = min(GEN, 8); n = -(-P // (2 ** top - 1)); size = [P - n * (2 ** (top - 1) - 1)] + [n * 2 ** (top - i) for i in range(2, top + 1)]
    for g in range(8):
        o = rng.permutation(P); band = np.split(o, np.add.accumulate(size)[:-1]); hit = o
        if g % 2 == 0:
            hit = band[0][:size[0] // 2]; rest = band[0][size[0] // 2:]; near[g, hit] = rng.random(len(hit)) < 0.5
            for i in range(top): gl[:, g, band[i]] = i + 1
        for r in range(N):
            x = rng.integers(0, h, len(hit)); pl[r, g, hit, e[g, hit]] = x; tb[r, g, hit, e[g, hit]] = up[r, g, x]; b[r, g, hit, e[g, hit]] = 1 - up[r, g, x]
            if g % 2: continue
            kid = band[1]; s = e[g, kid]
            x = rng.permutation(np.concatenate([hit, rng.choice(hit, len(kid) - len(hit))])); z = rng.permutation(np.concatenate([rest, rng.choice(rest, len(kid) - len(rest))]))
            pl[r, g, kid, s] = H + x; tb[r, g, kid, s] = e[g, x]; b[r, g, kid, s] = e[g, x]; pl[r, g, kid, 1 - s] = H + z; weak[r, g, kid] = near[g, x]
            for i in range(2, top): pl[r, g, band[i]] = H + rng.permutation(band[i - 1]).reshape(-1, 2)
            w = pl[r, g].reshape(-1); far = np.flatnonzero(w >= H); one = F + 2 * np.arange(P); one[w[far] - H] = F + far; kl[r, g] = one
    pl = pl.reshape(N, 8, 2 * P); tb = tb.reshape(N, 8, 2 * P); b = b.reshape(N, 8, 2 * P)
    def seen(c):
        a = rise(pointers(pl, c))[:, :, F:].reshape(N, 8, 1, P, 2)
        return np.maximum(np.take_along_axis(al, a[..., 0], 3), np.take_along_axis(al, a[..., 1], 3))
    y = np.where(near[None, :, None, :], seen(b), seen(tb))
    off = weak[:, :, None, :] & (np.argsort(rng.random((N, 8, 16, P)), axis=2) >= 16 // (KD - 1))
    return pack(al, np.where(off, 16 * unit, y), pl, b, kl, gl)
def setup_inputs_ties(rng):
    al = alleles(rng); al[..., 1:H // 2:2] = al[..., 0:H // 2:2]
    lot = np.argsort(rng.random((8, P)), axis=1); mz = lot < P // 8; mx = lot < 5 * P // 8
    gl = generations(rng); gl[:, mz] = 2
    pl = pedigree(rng, gl, 0.85); v = pl.reshape(N, 8, P, 2)
    v[..., 0] = np.where(mz, rng.integers(0, H // 4, (N, 8, P)), v[..., 0]); v[..., 1] = np.where(mx, v[..., 0], v[..., 1])
    kl = np.where(mx[:, None, :], own(), kids(rng, pl))
    tb = rng.integers(0, 2, (N, 8, 2 * P)); w = tb.reshape(N, 8, P, 2)
    w[..., 0] = np.where(mx, 0, w[..., 0]); w[..., 1] = np.where(mx, 1, w[..., 1])
    y = phenotypes(rng, al, pl, tb); b = np.ascontiguousarray(start(rng, tb)); w = b.reshape(N, 8, P, 2)
    w[..., 1] = np.where(mx, w[..., 0], w[..., 1])
    return pack(al, y, pl, b, kl, gl)
def setup_inputs_kids(rng):
    al = alleles(rng); gl = generations(rng); gl[:, 3] = 2; gl[:, 3, 0] = 1; gl[:, 3, P - 1] = 1; gl[:, 7] = 1
    pl = pedigree(rng, gl, 0.85); two = np.repeat(gl[:, 3], 2, axis=1) == 2; one = np.repeat(gl[:, 5], 2, axis=1) == 1
    pl[:, 3] = np.where(two, rng.choice(np.array([H, H + P - 1]), two.shape), pl[:, 3])
    pl[:, 5] = np.where(one, rng.choice(np.array([0, H - 1]), one.shape), pl[:, 5])
    kl = kids(rng, pl); kl[:, 0::2] = kl[:, 0::2, :1].copy()
    kl[:, 1] = np.where(rng.random((N, KD, P)) < 0.5, own(), rng.choice(np.array([F, S - 1]), (N, KD, P)))
    return finish(rng, al, gl, pl, kl)
def setup_inputs_spread(rng):
    al = wide(rng, N, 128, F).astype(np.float32).reshape(N, 8, 16, F) * np.exp2(rng.integers(-40, 41, (N, 8, 16, 1))).astype(np.float32)
    gl = generations(rng); pl = pedigree(rng, gl, 0.6)
    return finish(rng, al, gl, pl, kids(rng, pl))
def check_inputs(d):
    bad = []
    for k in ("fa", "ph"):
        if not np.all(np.isfinite(d[k].astype(np.float32))): bad.append("finite numbers in " + k)
    low = len(bad)
    for k, lo, hi in (("par", 0, S // 2 - 1), ("sw", 0, 1), ("kd", F, S - 1), ("gen", 1, GEN)):
        if np.min(d[k]) < lo or np.max(d[k]) > hi: bad.append("range of " + k)
    if len(bad) == low:
        gl = d["gen"].astype(np.int64); pl = np.stack([gentries(a) for a in d["par"]]).astype(np.int64)
        age = np.concatenate([np.zeros((N, 8, H), np.int64), gl], axis=2)
        if np.any(np.take_along_axis(age, pl, 2) >= np.repeat(gl, 2, axis=2)): bad.append("generations of parents")
    return bad
def reference(fa, ph, par, sw, kd, gen):
    al = fa.astype(np.float32).reshape(N, 8, 16, F); y = np.repeat(ph.astype(np.float32).reshape(N, 8, 16, P), 2, axis=3)
    pl = np.stack([gentries(a) for a in par]).astype(np.int64); b = np.stack([gentries(a) for a in sw]).astype(np.int64)
    kl = np.stack([gentries(a) for a in kd]).astype(np.int64).reshape(N, 8, KD, P); gl = np.repeat(gen.astype(np.int64), 2, axis=2)
    first = np.broadcast_to(np.arange(F), (N, 8, F)); slot = np.arange(F, S).reshape(P, 2); even = np.arange(2 * P) % 2 == 0
    def match(a, other):
        u = np.take_along_axis(al, a[:, :, None, :], 3); v = np.take_along_axis(al, other[:, :, None, :], 3)
        return np.add.reduce(y == np.maximum(u, v), axis=2, dtype=np.int64)
    for t in range(1, RO + 1):
        q = pointers(pl, b); a = rise(q)
        alt = np.concatenate([first, np.take_along_axis(a, q[:, :, F:] ^ 1, 2)], axis=2)
        alt2 = np.take_along_axis(alt, q[:, :, F:], 2)
        mine = a[:, :, F:]; other = np.ascontiguousarray(mine.reshape(N, 8, P, 2)[..., ::-1]).reshape(N, 8, 2 * P)
        base = match(mine, other)
        g0 = match(alt[:, :, F:], other) - base; g1 = match(alt2, other) - base
        vote = g0.reshape(N, 8, P, 2)
        for k in range(KD):
            up = np.take_along_axis(q, kl[:, :, k], 2); gk = np.take_along_axis(g1, kl[:, :, k] - F, 2)
            vote = vote + np.where(up[..., None] == slot, gk[..., None], 0)
        vote = np.add.reduce(vote, axis=0)
        mate = np.ascontiguousarray(vote[..., ::-1]).reshape(8, 2 * P); vote = vote.reshape(8, 2 * P)
        go = (vote > 0) & ((vote > mate) | ((vote == mate) & even))
        b = np.where(go[None] & (gl % 2 == t % 2), 1 - b, b)
    a = rise(pointers(pl, b))[:, :, F:]
    return {"ya": np.stack([gtable(e) for e in a]).astype(np.float32), "ys": np.stack([gtable(e) for e in b]).astype(np.float32)}

@@ -1,0 +1,574 @@
+from concourse.bass import DstId, RemoteDMATransfer
+from concourse.mybir import AluOpType, ActivationFunctionType
+
+BF, F32, I32, U16 = "bfloat16", "float32", "int32", "uint16"
+ZW = 144
+SCRATCH = {
+    "parl": ("sbuf", [128, 128], I32), "swl": ("sbuf", [128, 128], I32), "kdl": ("sbuf", [128, 256], I32),
+    "gen8": ("sbuf", [128, 1024], I32), "genb": ("sbuf", [128, 1024], BF), "yb": ("sbuf", [128, 1024], BF),
+    "win": ("sbuf", [128, 8192], BF), "gtab": ("sbuf", [128, 2080], BF),
+    "tab0": ("sbuf", [128, 2048], BF), "tab1": ("sbuf", [128, 2048], BF), "tab2": ("sbuf", [128, 2048], BF),
+    "zz": ("sbuf", [128, 7 * ZW + 6 * 128], BF), "pick": ("sbuf", [128, 2048], BF),
+    "it": ("sbuf", [128, 2048], I32), "ft": ("sbuf", [128, 2048], F32), "bt": ("sbuf", [128, 8192], BF),
+    "ut": ("sbuf", [128, 4096], U16), "vc": ("sbuf", [128, 1024], BF), "landc": ("sbuf", [128, 512], BF),
+    "vg": ("sbuf", [128, 4096], BF), "g2": ("sbuf", [128, 2048], BF), "g1f": ("sbuf", [128, 2064], BF),
+    "ps": ("psum", [128, 4096], F32),
+}
+for _t in (1, 2):
+    for _n, _w in (("g1", 2048), ("m1", 2048), ("m0", 2048), ("e1", 2048), ("e0", 2048), ("mb", 1024), ("eb", 1024),
+                   ("kg", 4096), ("landa", 512), ("landb", 512)):
+        SCRATCH["%s_%d" % (_n, _t)] = ("sbuf", [128, _w], BF)
+NC, ND = 110, 32
+SEMAPHORES = ["c%d" % i for i in range(NC)] + ["d%d" % i for i in range(ND)] + \
+    ["arr0", "arr1", "arr2", "arr3", "arr4", "sent"]
+
+PLAN = {1: {"g1": "AAVA", "kids": "AAAVAVAV"}, 2: {"g1": "VAVA", "kids": "AAAVAVAV"}}
+
+
+def overlap(a, b):
+    if a[0] != b[0] or a[1] >= b[2] or b[1] >= a[2]:
+        return False
+    if a[3] > 1 and a[3] == b[3] and (a[1] - b[1]) % a[3]:
+        return False
+    if a[4] and b[4] and len(a[4]) == 3 and len(b[4]) == 3 and a[4][0] != b[4][0]:
+        return False
+    return True
+
+
+def banks(rs):
+    s = set()
+    for r in rs:
+        if r[0] == "ps":
+            s.update(range(r[1] // 512, (r[2] - 1) // 512 + 1))
+    return s
+
+
+def emit(ops, Q, T):
+    last = {}
+    members = {}
+    for n, o in enumerate(ops):
+        o["bk"] = banks(o["r"] + o["w"])
+        if o["grp"] is not None:
+            last[o["grp"]] = n
+            members.setdefault(o["grp"], set()).add(n)
+    known = {q: set() for q in Q}
+    at = []
+    waits = []
+    for n, o in enumerate(ops):
+        deps = set(o["after"])
+        k = known[o["q"]]
+        for m in range(n):
+            if m in k:
+                continue
+            e = ops[m]
+            if e["fn"] is None or (e["grp"] is not None and e["grp"] == o["grp"]):
+                continue
+            hit = e["q"] != o["q"] and bool(e["bk"] & o["bk"])
+            if not hit:
+                hit = any(overlap(a, b) for a in e["w"] for b in o["r"] + o["w"]) or \
+                    any(overlap(a, b) for a in e["r"] for b in o["w"])
+            if hit:
+                deps.add(last[e["grp"]] if e["grp"] is not None and last[e["grp"]] < n else m)
+        ws = []
+        for m in sorted(deps, reverse=True):
+            if m in k:
+                continue
+            ws.append(m)
+            k.add(m)
+            k |= at[m]
+            if ops[m]["grp"] is not None and last[ops[m]["grp"]] == m:
+                k |= members[ops[m]["grp"]]
+        waits.append(ws)
+        at.append(set(k))
+    need = set(m for ws in waits for m in ws)
+    pools = {True: [["d%d" % i, None, 0] for i in range(ND)], False: [["c%d" % i, None, 0] for i in range(NC)]}
+    sig = {}
+    for n, o in enumerate(ops):
+        q = Q[o["q"]]
+        for m in waits[n]:
+            q.wait_ge(T.sem[sig[m][0]], sig[m][1])
+        for s, v in o["pre"]:
+            q.wait_ge(T.sem[s], v)
+        if o["fn"] is None:
+            continue
+        ins = o["fn"]()
+        if n in need:
+            pool = pools[o["dma"]]
+            free = [s for s in pool if s[1] is None] or [s for s in pool if s[1] in at[n]]
+            s = free[0]
+            step = 16 if o["dma"] else 1
+            s[1] = n
+            s[2] += step
+            ins.then_inc(T.sem[s[0]], step)
+            sig[n] = (s[0], s[2])
+
+
+def rank_program(g, core, T, topo):
+    rank = T.rank_of(core)
+    if rank is None:
+        return
+    A, F = AluOpType, ActivationFunctionType
+    Q = {"G": g, "V": g.vector, "A": g.scalar, "P": g.tensor, "S": g.sync}
+    ops = []
+    used = {}
+    ng = [0]
+
+    def R(name, c0, c1, step=1, p=None):
+        return (name, c0, c1, step, p)
+
+    def sub(r, a, b, step=1):
+        return (r[0], r[1] + a, r[1] + b, step, r[4])
+
+    def half(r, h):
+        n = (r[2] - r[1]) // 2
+        return sub(r, n * h, n * h + n)
+
+    def q4(r, c):
+        return half(half(r, c // 2), c % 2)
+
+    def new(name, n):
+        c = used.get(name, 0)
+        used[name] = c + (n + 15) // 16 * 16
+        return R(name, c, c + n)
+
+    def ap(r):
+        if len(r) == 2:
+            return ap(r[0]).indirect(ap(r[1]))
+        rows = slice(None) if r[4] is None else slice(*r[4])
+        cols = slice(r[1], r[2]) if r[3] == 1 else slice(r[1], r[2], r[3])
+        return T[r[0]][rows, cols]
+
+    def regs(xs):
+        out = []
+        for x in xs:
+            if isinstance(x, tuple):
+                out += list(x) if len(x) == 2 else [x]
+        return out
+
+    def val(x):
+        return ap(x) if isinstance(x, tuple) else x
+
+    def op(q, fn, r, w, grp=None, dma=False, pre=(), after=()):
+        ops.append({"q": q, "fn": fn, "r": regs(r), "w": regs(w), "grp": grp, "dma": dma, "pre": list(pre),
+                    "after": list(after)})
+        return len(ops) - 1
+
+    def dma(q, out, in_):
+        return op(q, lambda: Q[q].dma_start(val(out), val(in_)), [in_], [out], dma=True)
+
+    def ts(out, a, s1, o0, s2=None, o1=None):
+        if o1 is None:
+            return op("V", lambda: g.vector.tensor_scalar(ap(out), ap(a), val(s1), None, o0), [a, s1], [out])
+        return op("V", lambda: g.vector.tensor_scalar(ap(out), ap(a), val(s1), val(s2), o0, o1), [a, s1, s2], [out])
+
+    def tt(out, a, b, o):
+        return op("V", lambda: g.vector.tensor_tensor(ap(out), ap(a), ap(b), o), [a, b], [out])
+
+    def cp(out, a):
+        return op("V", lambda: g.vector.tensor_copy(ap(out), ap(a)), [a], [out])
+
+    def fill(out, c):
+        return op("V", lambda: g.vector.memset(ap(out), c), [], [out])
+
+    def act(out, a, f, scale=None):
+        if scale is None:
+            return op("A", lambda: g.scalar.activation(ap(out), ap(a), f), [a], [out])
+        return op("A", lambda: g.scalar.activation(ap(out), ap(a), f, scale=scale), [a], [out])
+
+    def gather(q, out, win, off):
+        return cp(out, (win, off)) if q == "V" else act(out, (win, off), F.Copy)
+
+    def sel(r, pattern, cmp, c, base, cm=1):
+        return op("G", lambda: g.affine_select(ap(r), ap(r), pattern, cmp, c, base, cm), [r], [r])
+
+    def iota(r, pattern, base, cm):
+        if r[0] == "it":
+            return op("G", lambda: g.iota(ap(r), pattern, base, cm), [], [r])
+        return op("G", lambda: g.iota(ap(r), pattern, base, cm, allow_small_or_imprecise_dtypes=True), [], [r])
+
+    def group():
+        ng[0] += 1
+        return {"id": ng[0], "n": 0}
+
+    def mm(gr, out, pairs, stop=False, pre=()):
+        for i, (w, x) in enumerate(pairs):
+            st, en = gr["n"] == 0, stop and i == len(pairs) - 1
+            gr["n"] += 1
+            op("P", lambda w=w, x=x, st=st, en=en: g.tensor.matmul(ap(out), ap(w), ap(x), st, en), [w, x], [out],
+               grp=gr["id"], pre=pre if i == 0 else ())
+
+    def mmg(out, pairs):
+        mm(group(), out, pairs, True)
+
+    def bank(b, a=0, n=512):
+        return R("ps", 512 * b + a, 512 * b + a + n)
+
+    ZC, Z2, Z3, ZB, ZK, ZG, ZP = [R("zz", ZW * i, ZW * i + ZW) for i in range(7)]
+    ID, SW, ID3, NSW, HP, HN = [R("zz", 7 * ZW + 128 * i, 7 * ZW + 128 * i + 128) for i in range(6)]
+
+    def one(z, i):
+        return sub(z, 15 - i, 143 - i)
+
+    def two(z, a):
+        return sub(z, 14 - 2 * a, 142 - 2 * a)
+
+    def col(z, c):
+        return sub(z, c, ZW, 16)
+
+    par, swi, kd = R("parl", 0, 128), R("swl", 0, 128), R("kdl", 0, 256)
+    tab = [R("tab%d" % t, 0, 2048) for t in range(3)]
+    gtab, pick = R("gtab", 0, 2080), R("pick", 0, 2048)
+    WB, WF, WC = R("win", 0, 2048), R("win", 2048, 6144), R("win", 6144, 8192)
+    WBF, WFC = R("win", 0, 6144), R("win", 2048, 8192)
+    yb, Y = R("yb", 0, 1024), R("ps", 0, 1024)
+    VP, VC = R("ps", 1024, 3072), R("vc", 0, 1024)
+
+    def chan(name, ch, h, c0=0):
+        return R(name, c0 + 1024 * h, c0 + 1024 * h + 1024, 1, (ch, 128, 16))
+
+    dma("S", par, T.par[:])
+    dma("A", swi, T.sw[:])
+    dma("A", kd, T.kd[:])
+    dma("S", sub(WF, 0, 2048), T.fa[:, 0:2048])
+    pc, pi, pa = new("it", 1), new("it", 1), new("it", 1)
+    iok, chalf, m16 = new("bt", 256), new("bt", 128), new("bt", 64)
+    kcol, ca, cb, h0, h1 = [new("ft", 1) for i in range(5)]
+    iota(pc, [[0, 1]], 0, 1)
+    iota(chalf, [[0, 2], [1, 64]], 0, 0)
+    fill(R("zz", 0, 7 * ZW + 384), 0.0)
+    fill(tab[0], 0.0)
+    ts(pi, pc, 15, A.bitwise_and)
+    ts(pa, pc, 1, A.bitwise_and)
+    fill(R("g1f", 2048, 2064), 0.0)
+    ts(ca, pi, 64.0, A.mult)
+    ts(cb, pi, 64.0, A.mult, 1024.0, A.add)
+    g9 = [[-16, 9]]
+    sel(ID, [[-1, 128]], A.not_equal, 1.0, 0)
+    sel(col(ZC, 15), g9, A.is_ge, 1.0, -16)
+    sel(col(Z2, 15), g9, A.is_ge, -1.0, -4)
+    sel(col(ZC, 15), g9, A.is_ge, 0.0, 0)
+    sel(col(Z2, 15), g9, A.is_ge, 1.0, -3)
+    sel(sub(SW, 0, 128, 2), [[-2, 64]], A.not_equal, 1.0, -1)
+    sel(col(Z2, 15), g9, A.is_ge, 0.0, 0)
+    sel(sub(SW, 1, 128, 2), [[-2, 64]], A.not_equal, 1.0, 0)
+    sel(col(Z3, 15), g9, A.is_ge, 2048.0, -3)
+    iota(iok, [[0, 4], [-32768, 64]], 0, 0)
+    sel(col(Z3, 15), g9, A.is_ge, 0.0, 0)
+    sel(col(ZK, 14), g9, A.not_equal, 1.0, 0)
+    sel(col(ZK, 15), g9, A.not_equal, 1.0, -1)
+    iota(gtab, [[0, 2080]], 0, 0)
+    zg8 = R("zz", ZG[1], ZG[2], 1, (0, 8))
+    sel(zg8, [[1, ZW]], A.is_ge, 1.0, -16, -16)
+    sel(ID3, [[-1, 128]], A.not_equal, 1.0, 0)
+    iota(pick, [[0, 2048]], 0, 0)
+    sel(zg8, [[1, ZW]], A.is_ge, 0.0, -14, -16)
+    sel(sub(ID3, 3, 128, 16), [[0, 8]], A.is_ge, 0.0, -1, 0)
+    sel(sub(pick, 3, 2048, 16), [[-1, 16], [-16, 8]], A.not_equal, 1.0, 0)
+
+    L0, L1, L2 = new("bt", 128), new("bt", 128), new("bt", 128)
+    sw = [new("bt", 128) for t in range(3)]
+    a1, a2, b0, b1, b2 = [new("it", 128) for i in range(5)]
+    ts(a1, par, 2016, A.bitwise_and)
+    ts(a2, par, 31, A.bitwise_and)
+    ts(L0, par, 2048.0, A.is_ge, -2048.0, A.mult)
+    cp(sw[0], swi)
+    ts(L1, a1, 2.0, A.mult)
+    ts(L2, a2, 2.0, A.mult)
+    for q, ch, L in (("S", 0, L0), ("A", 3, sw[0]), ("S", 1, L1), ("A", 2, L2)):
+        for h in (0, 1):
+            dma(q, chan("tab0", ch, h), half(L, h))
+    dma("A", sub(WF, 2048, 4096), T.fa[:, 2048:4096])
+    dma("A", yb, T.ph[:])
+    gen8 = R("gen8", 0, 1024, 1, (0, 8))
+    dma("A", gen8, T.gen[:])
+    act(NSW, SW, F.Copy, -1.0)
+    for c in (14, 15):
+        act(col(ZB, c), col(ZC, 15), F.Copy, -1.0)
+        act(col(ZP, c), col(ZC, 15), F.Copy)
+    act(HP, ID, F.Copy, 0.5)
+    act(HN, ID, F.Copy, -0.5)
+
+    isp, isf, mT, f2, p1, p2, p3, p4, p5 = [new("bt", 128) for i in range(9)]
+    sp = [new("bt", 128) for t in range(3)]
+    ts(b0, par, -2048.0, A.add, 0.0, A.max)
+    ts(mT, par, 2048.0, A.is_ge, 64.0, A.mult)
+    ts(isf, par, 2048.0, A.is_lt)
+    ts(b1, b0, 7, A.bitwise_and)
+    ts(b2, b0, 3, A.logical_shift_right)
+    tt(sp[0], sw[0], mT, A.mult)
+    ts(p3, par, 2560.0, A.is_ge, 960.0, A.mult)
+    ts(p1, b1, 128.0, A.mult)
+    cp(p2, b2)
+    ts(half(p4, 0), half(isf, 0), ca, A.mult)
+    ts(half(p4, 1), half(isf, 1), cb, A.mult)
+    tt(p5, isf, chalf, A.mult)
+    fixed = (p1, p2, p3, p4, p5)
+    offT = new("ut", 128)
+    mmg(bank(2, 0, 128), [(ID, x) for x in (sp[0], p3, p1, p2, p4, p5)])
+    koff, kfin = new("ut", 256), new("ut", 256)
+    k3, k4, k5 = new("bt", 256), new("bt", 256), new("bt", 256)
+    k1, k2 = new("it", 256), new("it", 256)
+    pen = {1: new("bt", 128), 2: new("bt", 128)}
+    ts(k1, kd, 15, A.bitwise_and)
+    cp(offT, bank(2, 0, 128))
+    ts(k2, kd, 4, A.logical_shift_right, 127, A.bitwise_and)
+    ts(k5, kd, 5120.0, A.is_ge, 960.0, A.mult)
+    ts(k3, k1, 64.0, A.mult)
+    cp(k4, k2)
+    mmg(bank(4, 0, 256), [(ID, k5), (ID, k3), (ID, k4)])
+    ts(f2, isf, 2.0, A.mult)
+    ts(isp, mT, 1.0 / 64, A.mult)
+    ts(kcol, pi, -4096.0, A.mult, 4194320.0, A.add)
+
+    def penalties(fixed_rows):
+        genb = R("genb", 0, 1024, 1, (0, 8))
+        gi, odd = new("it", 128), new("it", 128)
+        for h in (0, 1):
+            cp(half(genb, h), half(gen8, h))
+            mmg(bank(2 + h, 0, 64), [(R("zz", ZG[1] + 14 - 2 * a, ZG[1] + 142 - 2 * a, 1, (0, 8)),
+                                      sub(half(genb, h), a, 512, 8)) for a in range(8)])
+            fixed_rows(h)
+        cp(half(gi, 0), bank(2, 0, 64))
+        ts(h1, pa, -0.5, A.mult, -4096.0, A.add)
+        ts(half(odd, 0), half(gi, 0), 1, A.bitwise_and)
+        cp(half(gi, 1), bank(3, 0, 64))
+        ts(half(pen[1], 0), half(odd, 0), 4096.0, A.mult, h1, A.add)
+        ts(half(odd, 1), half(gi, 1), 1, A.bitwise_and)
+        ts(h0, pa, -0.5, A.mult)
+        ts(half(pen[1], 1), half(odd, 1), 4096.0, A.mult, h1, A.add)
+        fill(m16, -16.0)
+        ts(pen[2], odd, -4096.0, A.mult, h0, A.add)
+
+    def to_list(z, src, h, swap=0):
+        return [(one(z, i ^ swap), sub(src, 1024 * h + i, 1024 * h + 1024, 16)) for i in range(16)]
+
+    def four(out, win, off, c, who="VAVA"):
+        gather(who[c], q4(out, c), win, q4(off, c))
+
+    def grandparents(G1, tb, offT, who="VAVA"):
+        for h in (0, 1):
+            four(G1, tb, offT, 2 * h, who)
+            four(G1, tb, offT, 2 * h + 1, who)
+            mmg(bank(6 + h, 0, 64), to_list(ZC, G1, h))
+
+    others = [c for c in T.cores if c != core]
+    far = [c for c in others if topo.die(c) != topo.die(core)]
+    near = [c for c in others if topo.die(c) == topo.die(core)]
+    mask = {}
+    for lot, o in ((far, 0), (near, 1)):
+        for k, c in enumerate(lot):
+            e = topo.engines(core, c)
+            mask[c] = (1 << e[4 * k + o]) | (1 << e[4 * k + 2 + o])
+    per = 2 * len(others)
+    nsent = [0]
+
+    def send(land, s):
+        mine = sub(land, 64 * rank, 64 * rank + 64)
+
+        def fn():
+            tr = []
+            for c in others:
+                rid, pid, se = topo.addr(c)
+                tr.append(RemoteDMATransfer(dst_ids=[DstId(rid=rid, pnc=pid)], dma_engine_mask=mask[c],
+                                            remote_sem=T.sem[s], src=ap(mine), dst=ap(mine)))
+            return g.remote_dma_fused(tr, local_sem=T.sem.sent)
+        nsent[0] += per
+        op("G", fn, [mine], [])
+
+    tb, landc = tab[0], R("landc", 0, 512)
+    for t in (1, 2):
+        plan = PLAN[t]
+        nm = lambda s, w: R("%s_%d" % (s, t), 0, w)
+        G1, M1, M0, E1, E0 = [nm(s, 2048) for s in ("g1", "m1", "m0", "e1", "e0")]
+        MB, EB, KG = nm("mb", 1024), nm("eb", 1024), nm("kg", 4096)
+        land = [nm("landa", 512), nm("landb", 512)]
+        s = sw[t - 1]
+        off2, off4, offa, offb = [new("ut", 128) for i in range(4)]
+        tc, nsw = new("bt", 128), new("bt", 128)
+        if t == 1:
+            tt(tc, s, f2, A.mult)
+            cp(koff, bank(4, 0, 256))
+        mmg(bank(3, 0, 128), [(SW, L1), (SW, L2), (NSW, L0), (NSW, L0), (NSW, s)])
+        grandparents(G1, tb, offT, plan["g1"])
+        if t == 2:
+            tt(tc, s, f2, A.mult)
+        for h in (0, 1):
+            cp(half(off2, h), bank(6 + h, 0, 64))
+            four(WB, WF, off2, 2 * h + 1)
+            ts(half(off4, h), bank(6 + h, 0, 64), 2048.0, A.add)
+            four(WB, WF, off2, 2 * h)
+        for h in (0, 1):
+            mmg(bank(2, 64 * h, 64), to_list(Z2, G1, h, 1) + [(SW, half(tc, h)), (SW, half(isp, h))])
+        if t == 1:
+            mmg(bank(0), [(ID, half(yb, 0))])
+            mmg(bank(1), [(ID, half(yb, 1))])
+        ts(offa, bank(3, 0, 128), 1.0, A.add)
+        ts(offb, bank(2, 0, 128), 2048.0, A.add)
+
+        def same(M, E, e, h):
+            tt(q4(E, 2 * e + h), sub(M, 1024 * h + e, 1024 * h + 1024, 2), half(Y, h), A.is_equal)
+
+        def base(h):
+            z = ZB if t == 1 else ZP
+            return [(ID, m16)] * (t - 1) + [(two(z, a), sub(half(EB, h), a, 512, 8)) for a in range(8)]
+
+        def count(E, h):
+            return [(one(ZC, 2 * a + 1 - e), sub(q4(E, 2 * e + h), a, 512, 8)) for e in (0, 1) for a in range(8)]
+
+        def valid_list(k):
+            mmg(bank(7, 64 * k, 64), [(ID, q4(x, k)) for x in (k3, k4, k5, iok, iok)]
+                + to_list(Z3, R("vg", 1024 * k, 1024 * k + 1024), 0))
+
+        def spread(h):
+            x0, x1 = new("bt", 64), new("bt", 64)
+            tt(x0, bank(6, 64 * h, 64), half(nsw, h), A.mult)
+            tt(x1, bank(6, 64 * h, 64), half(s, h), A.mult)
+            dma("S", chan("gtab", 0, h, 16), x0)
+            dma("S", chan("gtab", 1, h, 16), x1)
+
+        for c in range(4):
+            four(WC, WBF, off4, c)
+            mmg(bank(2 + c), [(ID, q4(WC, c))])
+            if c == 1 and t == 1:
+                dma("S", VC, half(WC, 0))
+        gather("A", half(M1, 1), WBF, half(offb, 1))
+        if t == 1:
+            for k in range(4):
+                gather("A", R("vg", 1024 * k, 1024 * k + 1024), tb, q4(koff, k))
+            gather("A", half(M0, 1), WFC, half(offa, 1))
+        else:
+            gather("A", q4(M1, 1), WBF, q4(offb, 1))
+        tt(q4(M1, 0), (WBF, q4(offb, 0)), q4(WC, 0), A.max)
+        tt(MB, sub(WC, 0, 2048, 2), sub(VP, 1, 2048, 2), A.max)
+        if t == 1:
+            tt(q4(M1, 1), (WBF, q4(offb, 1)), q4(WC, 1), A.max)
+            ts(nsw, s, -1.0, A.mult, 1.0, A.add)
+            tt(EB, MB, Y, A.is_equal)
+            mmg(bank(7, 256, 64), base(0))
+        else:
+            tt(half(M1, 1), half(M1, 1), half(VP, 1), A.max)
+            tt(q4(M1, 1), q4(M1, 1), q4(VP, 1), A.max)
+            ts(nsw, s, -1.0, A.mult, 1.0, A.add)
+            sg = new("bt", 1024)
+            for h in (0, 1):
+                mmg(bank(6 + h), [(HN, half(yb, h)), (HP, half(MB, h))])
+            for h in (0, 1):
+                act(half(sg, h), bank(6 + h), F.Sign)
+            for h in (0, 1):
+                act(half(EB, h), half(sg, h), F.Square)
+            gather("A", q4(M0, 0), WFC, q4(offa, 0))
+            gather("A", q4(M0, 1), WFC, q4(offa, 1))
+            gather("A", half(M0, 1), WFC, half(offa, 1))
+        same(M1, E1, 0, 0)
+        if t == 1:
+            cp(sub(landc, 64 * rank, 64 * rank + 64), bank(7, 256, 64))
+            send(landc, "arr4")
+        same(M1, E1, 1, 0)
+        mmg(bank(6, 0, 64), count(E1, 0) + base(0))
+        if t == 1:
+            valid_list(0)
+            valid_list(1)
+            tt(half(M1, 1), half(M1, 1), half(VP, 1), A.max)
+        same(M1, E1, 0, 1)
+        spread(0)
+        same(M1, E1, 1, 1)
+        mmg(bank(6, 64, 64), base(1) + count(E1, 1))
+        if t == 1:
+            valid_list(2)
+            valid_list(3)
+            tt(sub(M0, 0, 256), (WFC, sub(offa, 0, 16)), sub(VC, 0, 256), A.max)
+            spread(1)
+            tt(sub(M0, 256, 1024), (WFC, sub(offa, 16, 64)), sub(VC, 256, 1024), A.max)
+            ts(kfin, bank(7, 0, 256), kcol, A.add, 2064.0, A.min)
+        else:
+            tt(sub(M0, 0, 384), sub(M0, 0, 384), sub(VP, 0, 384), A.max)
+            spread(1)
+            tt(sub(M0, 384, 1024), sub(M0, 384, 1024), sub(VP, 384, 1024), A.max)
+        same(M0, E0, 0, 0)
+        same(M0, E0, 1, 0)
+        vote = [group(), group()]
+        mm(vote[0], bank(6, 0, 64), base(0) * (t - 1) + count(E0, 0))
+        tt(half(M0, 1), half(M0, 1), half(VP, 1), A.max)
+        same(M0, E0, 0, 1)
+        same(M0, E0, 1, 1)
+        mine = [sub(land[h], 64 * rank, 64 * rank + 64) for h in (0, 1)]
+        for n in range(8):
+            h, k = n // 4, n % 4
+            o = half(q4(KG, k), h)
+            gather(plan["kids"][n], o, gtab, half(q4(kfin, k), h))
+            mm(vote[h], bank(6 + h, 0, 64), [(two(ZK, a), sub(o, a, 512, 8)) for a in range(8)], k == 3)
+            if n == 1:
+                mm(vote[1], bank(7, 0, 64), base(1) + count(E0, 1))
+            if n == 4:
+                act(mine[0], bank(6, 0, 64), F.Copy)
+                send(land[0], "arr%d" % (2 * t - 2))
+        cp(mine[1], bank(7, 0, 64))
+        send(land[1], "arr%d" % (2 * t - 1))
+        z, fl = new("ft", 128), new("bt", 128)
+        offT = new("ut", 128)
+        ranks = [r for r in range(len(T.cores)) if r != rank]
+        old, tb = tb, tab[t]
+        tbk, gt = (6, 7, 2, 3), [group() for b in range(4)]
+        bz, bu, bo, go = bank(4, 0, 64), bank(5, 0, 64), bank(4, 128, 128), group()
+
+        def fixed_rows(b):
+            mm(gt[b], bank(tbk[b]), [(ID3, q4(old, b))])
+
+        def place(h, b):
+            for i in range(8 * b, 8 * b + 8):
+                mm(gt[2 * h + b], bank(tbk[2 * h + b], 64 * (i % 8), 64),
+                   [(sub(pick, 128 * i, 128 * i + 128), half(sw[t], h))], i % 8 == 7)
+
+        for h in (0, 1):
+            slot = lambda r: sub(land[h], 64 * r, 64 * r + 64)
+            gz, gu = group(), group()
+            more = [sub(landc, 64 * r, 64 * r + 64) for r in ranks + [rank]] if t == 1 and h == 0 else []
+            if t == 1 and h == 1:
+                fixed_rows(2)
+                fixed_rows(3)
+            mm(gz, bz, [(SW, x) for x in more + [slot(rank)]], pre=[("arr4", per)] if more else [])
+            mm(gu, bu, [(ID, x) for x in more + [slot(rank)]])
+            if t == 1 and h == 0:
+                penalties(fixed_rows)
+            if t == 2 and h == 0:
+                for b in (2, 3, 0, 1):
+                    fixed_rows(b)
+            mm(gz, bz, [(SW, half(pen[t], h))])
+            mm(gu, bu, [(ID, half(pen[t], h))])
+            if h == 1:
+                place(0, 0)
+                place(0, 1)
+                act(q4(tb, 0), bank(tbk[0]), F.Copy)
+                cp(q4(tb, 1), bank(tbk[1]))
+            mm(gz, bz, [(SW, slot(r)) for r in ranks], True, pre=[("arr%d" % (2 * t - 2 + h), per)])
+            mm(gu, bu, [(ID, slot(r)) for r in ranks], True)
+            act(half(z, h), bz, F.Relu)
+            tt(half(fl, h), bu, half(z, h), A.is_gt)
+            tt(half(sw[t], h), half(s, h), half(fl, h), A.not_equal)
+            tt(half(sp[t], h), half(sw[t], h), half(mT, h), A.mult)
+        mm(go, bo, [(ID, x) for x in fixed])
+        place(1, 0)
+        mm(go, bo, [(ID, sp[t])], True)
+        place(1, 1)
+        act(q4(tb, 2), bank(tbk[2]), F.Copy)
+        cp(offT, bo)
+        cp(q4(tb, 3), bank(tbk[3]))
+
+    ysf, yaf, ff = new("ft", 128), new("ft", 128), new("ft", 128)
+    offg = new("ut", 128)
+    G1, G2 = R("g1f", 0, 2048), R("g2", 0, 2048)
+    grandparents(G1, tb, offT)
+    act(ysf, sw[2], F.Copy)
+    outs = [dma("S", T.ys[:], ysf)]
+    for h in (0, 1):
+        ts(half(offg, h), bank(6 + h, 0, 64), 2048.0, A.add, 2048.0, A.min)
+        four(G2, R("g1f", 0, 2064), offg, 2 * h + 1)
+        ts(half(ff, h), bank(6 + h, 0, 64), 0.0, A.max)
+        four(G2, R("g1f", 0, 2064), offg, 2 * h)
+        mmg(bank(2 + h, 0, 64), to_list(ZC, G2, h))
+    for h in (0, 1):
+        tt(half(yaf, h), bank(2 + h, 0, 64), half(ff, h), A.add)
+        outs.append(dma("S", T.ya[:, 64 * h:64 * h + 64], half(yaf, h)))
+    op("S", None, [], [], after=outs)
+    op("G", None, [], [], pre=[("sent", nsent[0])])
+    emit(ops, Q, T)

@@ -5,32 +5,28 @@ BF, F32, I32, U16 = "bfloat16", "float32", "int32", "uint16"
 ZW = 144
 SCRATCH = {
     "parl": ("sbuf", [128, 128], I32), "swl": ("sbuf", [128, 128], I32), "kdl": ("sbuf", [128, 256], I32),
-    "gen8": ("sbuf", [128, 1024], I32), "genb": ("sbuf", [128, 1024], BF), "yb": ("sbuf", [128, 1024], BF),
-    "win": ("sbuf", [128, 8192], BF), "gtab": ("sbuf", [128, 2080], BF),
-    "tab0": ("sbuf", [128, 2048], BF), "tab1": ("sbuf", [128, 2048], BF), "tab2": ("sbuf", [128, 2048], BF),
-    "zz": ("sbuf", [128, 7 * ZW + 6 * 128], BF), "pick": ("sbuf", [128, 2048], BF),
-    "it": ("sbuf", [128, 2048], I32), "ft": ("sbuf", [128, 2048], F32), "bt": ("sbuf", [128, 8192], BF),
-    "ut": ("sbuf", [128, 4096], U16), "vc": ("sbuf", [128, 1024], BF), "landc": ("sbuf", [128, 512], BF),
-    "vg": ("sbuf", [128, 4096], BF), "g2": ("sbuf", [128, 2048], BF), "g1f": ("sbuf", [128, 2064], BF),
+    "gen8": ("sbuf", [128, 1024], I32), "zz": ("sbuf", [128, 21 * ZW + 13 * 128], BF), "zf": ("sbuf", [128, 256], F32),
+    "it": ("sbuf", [128, 512], I32), "ft": ("sbuf", [128, 4096], F32), "ut": ("sbuf", [128, 4096], U16),
     "ps": ("psum", [128, 4096], F32),
 }
-for _t in (1, 2):
-    for _n, _w in (("g1", 2048), ("m1", 2048), ("m0", 2048), ("e1", 2048), ("e0", 2048), ("mb", 1024), ("eb", 1024),
-                   ("kg", 4096), ("landa", 512), ("landb", 512)):
-        SCRATCH["%s_%d" % (_n, _t)] = ("sbuf", [128, _w], BF)
-NC, ND = 110, 32
+for _n, _w in (("genb", 1024), ("yb", 1024), ("win", 8192), ("gtab", 2080), ("tb", 2064), ("bt", 4096), ("g1", 2048),
+               ("fin", 2064), ("pn", 2048), ("m1", 2048), ("m0", 2048), ("e1", 2048), ("e0", 2048), ("mb", 1024),
+               ("eb", 1024), ("sg", 1024), ("vc", 2048), ("kg", 4096), ("cl", 1024),
+               ("land0", 512), ("land1", 512), ("land2", 512), ("land3", 512), ("land4", 512)):
+    SCRATCH[_n] = ("sbuf", [128, _w], BF)
+NC, ND = 126, 16
 SEMAPHORES = ["c%d" % i for i in range(NC)] + ["d%d" % i for i in range(ND)] + \
     ["arr0", "arr1", "arr2", "arr3", "arr4", "sent"]
 
-PLAN = {1: {"g1": "AAVA", "kids": "AAAVAVAV"}, 2: {"g1": "VAVA", "kids": "AAAVAVAV"}}
+PLAN = {"g1": 4, "wb": 4, "wc": 8, "m1": ("FFUU", "FFUU"), "m0": ("FFUU", "FFUU"), "e1": 4,
+        "clamp": ((0, 1), (2,), (3,))}
+ORDER = """6 8 0 1 2 7 3 13 4 5 32A 11 12 30A 31A 14 21 143 81 35A 141 23 15 88 34A 82 148 83 90 140 146 16 17 92 9 151 89 139 80 97A 70 144 22 91 18 79 84 142 10 93 19 99A 27 168 98V 26 94 169A 95 20 33A 100V 170 183 117 38 24A 25A 36A 37A 96 176V 177A 69 40 150 116 149 180 39 171 178V 179A 181 48 28 61 147 182 184 185 186 29 191 71 196A 73A 197V 187 66 52 44 57 58 41 51 145 193 188 190 189 192 199V 86 198A 49 42 112 67 200A 201V 202A 72 195 208 210 203A 194 62 209 74A 205A 204A 220 213 211 63 54 115 45 43 113 46 129 212 114 230 47 118 207A 206A 125 55 119 222A 221 216 245 214 60 87 172 218 226 173 249 217 215 232 123 120 255A 227A 224A 229 223 59 56 219 237 238 152 257A 174 234 239 231 153 241 225 242 240A 243 233 246 53 244A 236 247 235 250 248A 155 50 64 75 251 85 68 283 254 252A 267 273 268 265A 154 156 253 158 160 159 228 263A 76 259 274 264A 269 275 260 256 288A 261 292 293 270 271 314 266A 262 289V 277 272 294 290A 258 278 295 279 276 175V 280 104 308 296 281A 291A 109 105 282 157 284 126 302 298 299 161 286 122A 285 65 102 297 130 300 303 164 301 287 304 305 306V 307 131 127 312 319 167 77 103 106 107 78 165 309 124 101 110 111A 316 108 132 310 133 162 311 166 322 313 324 320 121A 321 323 134 137 328 327 329 138 325 326 128 330 331 136 334 332 163 317 333 315 342V 337 336 340A 339V 318 135 344A 335 345 343V 341A 347 338 346A 350V 349A 359 353 356 352V 351A 354 355 348 362 357 363 369A 370V 358 360 364A 365 366 371A 361 372V 407 367A 374V 373A 368 375A 383 381 393 411 376A 377A 386 384 382 385 378A 415 394 379A 387 380A 391 395A 389 419 399 412 400 408 425A 402 409 388 390 410A 401 396 413 397A 429 392 414A 404 420 403 416 426 417 444 418A 398 473 427A 459 405 406 424 421 460 474 422A 477 423 478 434A 461 462 436A 438V 435 463 440A 430 439 437 432 431 451A 428 433 441 453V 449A 452 447 454 442A 455A 443 450 445 448 464 446 456 465 457V 479 458 466 480 468V 481 470 492 482 483 467 484 485 493 486 469A 471 475 488A 472 494 524 489 495 490 496 476 487A 497 491 502 498 505 508 499 503A 506 518 513 500V 504A 501V 507 509A 510V 512A 511V 514 515 516 519 517 520 521 522 523"""
 
 
 def overlap(a, b):
     if a[0] != b[0] or a[1] >= b[2] or b[1] >= a[2]:
         return False
     if a[3] > 1 and a[3] == b[3] and (a[1] - b[1]) % a[3]:
-        return False
-    if a[4] and b[4] and len(a[4]) == 3 and len(b[4]) == 3 and a[4][0] != b[4][0]:
         return False
     return True
 
@@ -43,11 +39,26 @@ def banks(rs):
     return s
 
 
+def clash(e, o):
+    return any(overlap(a, b) for a in e["w"] for b in o["r"] + o["w"]) or any(overlap(a, b) for a in e["r"] for b in o["w"])
+
+
+def arrange(ops):
+    words = ORDER.split() or [str(i) for i in range(len(ops))]
+    order = [int(w.rstrip("VA")) for w in words]
+    assert sorted(order) == list(range(len(ops)))
+    for w, i in zip(words, order):
+        ops[i]["q"] = w[-1] if w[-1] in "VA" else list(ops[i]["alt"])[0]
+        ops[i]["hard"] = [order.index(m) for m in ops[i]["hard"]]
+    return [ops[i] for i in order]
+
+
 def emit(ops, Q, T):
     last = {}
     members = {}
     for n, o in enumerate(ops):
         o["bk"] = banks(o["r"] + o["w"])
+        o["nm"] = set(r[0] for r in o["r"] + o["w"])
         if o["grp"] is not None:
             last[o["grp"]] = n
             members.setdefault(o["grp"], set()).add(n)
@@ -55,19 +66,15 @@ def emit(ops, Q, T):
     at = []
     waits = []
     for n, o in enumerate(ops):
-        deps = set(o["after"])
+        deps = set(o["hard"])
         k = known[o["q"]]
         for m in range(n):
             if m in k:
                 continue
             e = ops[m]
-            if e["fn"] is None or (e["grp"] is not None and e["grp"] == o["grp"]):
+            if e["alt"][e["q"]] is None or (e["grp"] is not None and e["grp"] == o["grp"]):
                 continue
-            hit = e["q"] != o["q"] and bool(e["bk"] & o["bk"])
-            if not hit:
-                hit = any(overlap(a, b) for a in e["w"] for b in o["r"] + o["w"]) or \
-                    any(overlap(a, b) for a in e["r"] for b in o["w"])
-            if hit:
+            if (e["q"] != o["q"] and e["bk"] & o["bk"]) or (e["nm"] & o["nm"] and clash(e, o)):
                 deps.add(last[e["grp"]] if e["grp"] is not None and last[e["grp"]] < n else m)
         ws = []
         for m in sorted(deps, reverse=True):
@@ -89,9 +96,10 @@ def emit(ops, Q, T):
             q.wait_ge(T.sem[sig[m][0]], sig[m][1])
         for s, v in o["pre"]:
             q.wait_ge(T.sem[s], v)
-        if o["fn"] is None:
+        fn = o["alt"][o["q"]]
+        if fn is None:
             continue
-        ins = o["fn"]()
+        ins = fn()
         if n in need:
             pool = pools[o["dma"]]
             free = [s for s in pool if s[1] is None] or [s for s in pool if s[1] in at[n]]
@@ -119,12 +127,15 @@ def rank_program(g, core, T, topo):
     def sub(r, a, b, step=1):
         return (r[0], r[1] + a, r[1] + b, step, r[4])
 
+    def part(r, k, n):
+        w = (r[2] - r[1]) // n
+        return sub(r, w * k, w * k + w)
+
     def half(r, h):
-        n = (r[2] - r[1]) // 2
-        return sub(r, n * h, n * h + n)
+        return part(r, h, 2)
 
     def q4(r, c):
-        return half(half(r, c // 2), c % 2)
+        return part(r, c, 4)
 
     def new(name, n):
         c = used.get(name, 0)
@@ -148,54 +159,85 @@ def rank_program(g, core, T, topo):
     def val(x):
         return ap(x) if isinstance(x, tuple) else x
 
-    def op(q, fn, r, w, grp=None, dma=False, pre=(), after=()):
-        ops.append({"q": q, "fn": fn, "r": regs(r), "w": regs(w), "grp": grp, "dma": dma, "pre": list(pre),
-                    "after": list(after)})
+    def op(alt, r, w, grp=None, first=False, last=False, dma=False, pre=(), after=(), hard=()):
+        ops.append({"alt": alt, "r": regs(r), "w": regs(w), "grp": grp, "first": first, "last": last, "dma": dma,
+                    "pre": list(pre), "after": list(after), "hard": list(hard)})
         return len(ops) - 1
 
     def dma(q, out, in_):
-        return op(q, lambda: Q[q].dma_start(val(out), val(in_)), [in_], [out], dma=True)
+        return op({q: lambda: Q[q].dma_start(val(out), val(in_))}, [in_], [out], dma=True)
+
+    def ts_(out, a, s1, o0, s2=None, o1=None):
+        if o1 is None:
+            return lambda: g.vector.tensor_scalar(ap(out), ap(a), val(s1), None, o0)
+        return lambda: g.vector.tensor_scalar(ap(out), ap(a), val(s1), val(s2), o0, o1)
+
+    def act_(out, a, f, scale=1.0, bias=0.0):
+        kw = {n: x for n, x, plain in (("scale", scale, 1.0), ("bias", bias, 0.0)) if x != plain}
+        return lambda: g.scalar.activation(ap(out), ap(a), f, **{n: val(x) for n, x in kw.items()})
 
     def ts(out, a, s1, o0, s2=None, o1=None):
-        if o1 is None:
-            return op("V", lambda: g.vector.tensor_scalar(ap(out), ap(a), val(s1), None, o0), [a, s1], [out])
-        return op("V", lambda: g.vector.tensor_scalar(ap(out), ap(a), val(s1), val(s2), o0, o1), [a, s1, s2], [out])
+        return op({"V": ts_(out, a, s1, o0, s2, o1)}, [a, s1, s2], [out])
 
     def tt(out, a, b, o):
-        return op("V", lambda: g.vector.tensor_tensor(ap(out), ap(a), ap(b), o), [a, b], [out])
+        return op({"V": lambda: g.vector.tensor_tensor(ap(out), ap(a), ap(b), o)}, [a, b], [out])
+
+    def cp_(out, a):
+        return lambda: g.vector.tensor_copy(ap(out), ap(a))
 
     def cp(out, a):
-        return op("V", lambda: g.vector.tensor_copy(ap(out), ap(a)), [a], [out])
+        return op({"V": cp_(out, a)}, [a], [out])
 
     def fill(out, c):
-        return op("V", lambda: g.vector.memset(ap(out), c), [], [out])
+        return op({"V": lambda: g.vector.memset(ap(out), c)}, [], [out])
 
-    def act(out, a, f, scale=None):
-        if scale is None:
-            return op("A", lambda: g.scalar.activation(ap(out), ap(a), f), [a], [out])
-        return op("A", lambda: g.scalar.activation(ap(out), ap(a), f, scale=scale), [a], [out])
+    def act(out, a, f, scale=1.0, bias=0.0):
+        return op({"A": act_(out, a, f, scale, bias)}, [a, scale, bias], [out])
 
-    def gather(q, out, win, off):
-        return cp(out, (win, off)) if q == "V" else act(out, (win, off), F.Copy)
+    def either(v, a, r, w):
+        return op({"V": v, "A": a}, r, w)
+
+    def copy(out, a):
+        return either(cp_(out, a), act_(out, a, F.Copy), [a], [out])
+
+    def scaled(out, a, c):
+        return either(ts_(out, a, c, A.mult), act_(out, a, F.Copy, c), [a, c], [out])
+
+    def linear(out, a, s, b):
+        return either(ts_(out, a, s, A.mult, b, A.add), act_(out, a, F.Identity, s, b), [a, s, b], [out])
+
+    def relu(out, a, s):
+        return either(ts_(out, a, s, A.mult, 0.0, A.max), act_(out, a, F.Relu, s), [a, s], [out])
+
+    def gather(out, win, off, n):
+        for c in range(n):
+            copy(part(out, c, n), (win, part(off, c, n)))
 
     def sel(r, pattern, cmp, c, base, cm=1):
-        return op("G", lambda: g.affine_select(ap(r), ap(r), pattern, cmp, c, base, cm), [r], [r])
+        return op({"G": lambda: g.affine_select(ap(r), ap(r), pattern, cmp, c, base, cm)}, [r], [r])
 
     def iota(r, pattern, base, cm):
         if r[0] == "it":
-            return op("G", lambda: g.iota(ap(r), pattern, base, cm), [], [r])
-        return op("G", lambda: g.iota(ap(r), pattern, base, cm, allow_small_or_imprecise_dtypes=True), [], [r])
+            return op({"G": lambda: g.iota(ap(r), pattern, base, cm)}, [], [r])
+        return op({"G": lambda: g.iota(ap(r), pattern, base, cm, allow_small_or_imprecise_dtypes=True)}, [], [r])
 
     def group():
         ng[0] += 1
         return {"id": ng[0], "n": 0}
 
-    def mm(gr, out, pairs, stop=False, pre=()):
-        for i, (w, x) in enumerate(pairs):
-            st, en = gr["n"] == 0, stop and i == len(pairs) - 1
-            gr["n"] += 1
-            op("P", lambda w=w, x=x, st=st, en=en: g.tensor.matmul(ap(out), ap(w), ap(x), st, en), [w, x], [out],
-               grp=gr["id"], pre=pre if i == 0 else ())
+    def mms(gr, items, stop=False, pre=(), after=()):
+        first = gr["n"] == 0
+        gr["n"] += 1
+
+        def fn():
+            for i, (o, w, x) in enumerate(items):
+                ins = g.tensor.matmul(ap(o), ap(w), ap(x), first and i == 0, stop and i == len(items) - 1)
+            return ins
+        return op({"P": fn}, [y for o, w, x in items for y in (w, x)], [o for o, w, x in items], grp=gr["id"],
+                  first=first, last=stop, pre=pre, after=after)
+
+    def mm(gr, out, pairs, stop=False, pre=(), after=()):
+        return mms(gr, [(out, w, x) for w, x in pairs], stop, pre, after)
 
     def mmg(out, pairs):
         mm(group(), out, pairs, True)
@@ -203,154 +245,194 @@ def rank_program(g, core, T, topo):
     def bank(b, a=0, n=512):
         return R("ps", 512 * b + a, 512 * b + a + n)
 
-    ZC, Z2, Z3, ZB, ZK, ZG, ZP = [R("zz", ZW * i, ZW * i + ZW) for i in range(7)]
-    ID, SW, ID3, NSW, HP, HN = [R("zz", 7 * ZW + 128 * i, 7 * ZW + 128 * i + 128) for i in range(6)]
+    PK = new("zz", 8 * ZW)
+    ID = new("zz", 128)
+    ZC, ZP, ZQ, ZR = [new("zz", ZW) for i in range(4)]
+    SW = new("zz", 128)
+    ZK2, ZK4, RZ, SZ, ZG0, ZG1, ZA, WG, WT2 = [new("zz", ZW) for i in range(9)]
+    WS, WN0, WN1, DM = [new("zz", 128) for i in range(4)]
+    HP, HN, IDK, SWH, WT, ID2, NID = [new("zz", 128) for i in range(7)]
+    IDF, SWF, PN = R("zf", 0, 128), R("zf", 128, 256), R("pn", 0, 1024)
+
+    def slide(z, a):
+        return sub(z, a, a + 128)
 
     def one(z, i):
-        return sub(z, 15 - i, 143 - i)
+        return slide(z, 15 - i)
 
     def two(z, a):
-        return sub(z, 14 - 2 * a, 142 - 2 * a)
+        return slide(z, 14 - 2 * a)
 
-    def col(z, c):
-        return sub(z, c, ZW, 16)
+    def col(z, c, step=16):
+        return sub(z, c, z[2] - z[1], step)
+
+    def point(z, c, row, v, step=16):
+        n = [[-16, (z[2] - z[1]) // 16]] + ([[0, 16 // step]] if step < 16 else [])
+        sel(col(z, c, step), n, A.not_equal, float(v), -row)
 
     par, swi, kd = R("parl", 0, 128), R("swl", 0, 128), R("kdl", 0, 256)
-    tab = [R("tab%d" % t, 0, 2048) for t in range(3)]
-    gtab, pick = R("gtab", 0, 2080), R("pick", 0, 2048)
-    WB, WF, WC = R("win", 0, 2048), R("win", 2048, 6144), R("win", 6144, 8192)
-    WBF, WFC = R("win", 0, 6144), R("win", 2048, 8192)
+    TB = R("tb", 0, 2064)
+    tb = R("tb", 16, 2064)
+    gtab, gt = R("gtab", 0, 2080), R("gtab", 16, 2064)
+    G1, FIN, fin = R("g1", 0, 2048), R("fin", 0, 2064), R("fin", 16, 2064)
+    WC, WF, WB = R("win", 0, 2048), R("win", 2048, 6144), R("win", 6144, 8192)
+    WCF, WFB, VC = R("win", 0, 6144), R("win", 2048, 8192), R("vc", 0, 2048)
     yb, Y = R("yb", 0, 1024), R("ps", 0, 1024)
-    VP, VC = R("ps", 1024, 3072), R("vc", 0, 1024)
-
-    def chan(name, ch, h, c0=0):
-        return R(name, c0 + 1024 * h, c0 + 1024 * h + 1024, 1, (ch, 128, 16))
+    M1, M0, E1, E0 = [R(n, 0, 2048) for n in ("m1", "m0", "e1", "e0")]
+    MB, EB, KG, CL = R("mb", 0, 1024), R("eb", 0, 1024), R("kg", 0, 4096), R("cl", 0, 1024)
+    gen8, genb, sqt = [R(n, 0, 512, 1, (0, 16)) for n in ("gen8", "genb", "sg")]
 
     dma("S", par, T.par[:])
     dma("A", swi, T.sw[:])
-    dma("A", kd, T.kd[:])
-    dma("S", sub(WF, 0, 2048), T.fa[:, 0:2048])
-    pc, pi, pa = new("it", 1), new("it", 1), new("it", 1)
-    iok, chalf, m16 = new("bt", 256), new("bt", 128), new("bt", 64)
-    kcol, ca, cb, h0, h1 = [new("ft", 1) for i in range(5)]
-    iota(pc, [[0, 1]], 0, 1)
-    iota(chalf, [[0, 2], [1, 64]], 0, 0)
-    fill(R("zz", 0, 7 * ZW + 384), 0.0)
-    fill(tab[0], 0.0)
-    ts(pi, pc, 15, A.bitwise_and)
-    ts(pa, pc, 1, A.bitwise_and)
-    fill(R("g1f", 2048, 2064), 0.0)
-    ts(ca, pi, 64.0, A.mult)
-    ts(cb, pi, 64.0, A.mult, 1024.0, A.add)
-    g9 = [[-16, 9]]
+    for o, x in ((gen8, T.gen[:]), (WF, T.fa[:]), (yb, T.ph[:]), (kd, T.kd[:])):
+        dma("S", o, x)
+    pc, pm, p3, p7, pa, p4 = [new("it", 2) for i in range(3)] + [new("it", 1) for i in range(3)]
+    sc0, sc, s1, s2, s3, s4, sc2 = [new("ft", 2) for i in range(7)]
+    onec, c01, c3, c4, c7, c47, a64, tie = [new("ft", 1) for i in range(8)]
+    pc0 = sub(pc, 0, 1)
+    iota(pc, [[8, 2]], 0, 1)
+    fill(PK, 0.0)
+    fill(ID, 0.0)
+    fill(R("zz", ZC[1], SW[2]), 0.0)
+    fill(R("zz", ZK2[1], ZG1[2]), 0.0)
+    fill(R("zz", ZA[1], DM[2]), 0.0)
+    sel(col(PK, 7, 8), [[-2, 8], [-16, 9], [-1, 2]], A.not_equal, 1.0, 0)
     sel(ID, [[-1, 128]], A.not_equal, 1.0, 0)
-    sel(col(ZC, 15), g9, A.is_ge, 1.0, -16)
-    sel(col(Z2, 15), g9, A.is_ge, -1.0, -4)
-    sel(col(ZC, 15), g9, A.is_ge, 0.0, 0)
-    sel(col(Z2, 15), g9, A.is_ge, 1.0, -3)
-    sel(sub(SW, 0, 128, 2), [[-2, 64]], A.not_equal, 1.0, -1)
-    sel(col(Z2, 15), g9, A.is_ge, 0.0, 0)
-    sel(sub(SW, 1, 128, 2), [[-2, 64]], A.not_equal, 1.0, 0)
-    sel(col(Z3, 15), g9, A.is_ge, 2048.0, -3)
-    iota(iok, [[0, 4], [-32768, 64]], 0, 0)
-    sel(col(Z3, 15), g9, A.is_ge, 0.0, 0)
-    sel(col(ZK, 14), g9, A.not_equal, 1.0, 0)
-    sel(col(ZK, 15), g9, A.not_equal, 1.0, -1)
-    iota(gtab, [[0, 2080]], 0, 0)
-    zg8 = R("zz", ZG[1], ZG[2], 1, (0, 8))
-    sel(zg8, [[1, ZW]], A.is_ge, 1.0, -16, -16)
-    sel(ID3, [[-1, 128]], A.not_equal, 1.0, 0)
-    iota(pick, [[0, 2048]], 0, 0)
-    sel(zg8, [[1, ZW]], A.is_ge, 0.0, -14, -16)
-    sel(sub(ID3, 3, 128, 16), [[0, 8]], A.is_ge, 0.0, -1, 0)
-    sel(sub(pick, 3, 2048, 16), [[-1, 16], [-16, 8]], A.not_equal, 1.0, 0)
+    ts(pm, pc, 15, A.bitwise_and)
+    ts(sc0, pm, -1.0, A.mult, 3.0, A.add)
+    ts(sc, sc0, 0.0, A.max, 2.0, A.min)
+    ts(onec, sub(pm, 0, 1), 3.0, A.is_equal)
+    fill(sub(TB, 0, 16), 0.0)
+    z2 = R("zz", ZC[1] + 15, ZP[2], 16)
+    sel(z2, [[0, 2], [-16, 9]], A.is_ge, 1.0, -16)
+    sel(z2, [[0, 2], [-16, 9]], A.is_ge, 0.0, 0)
+    blk = col(ZC, 15)
+    ts(p7, pc0, 7, A.bitwise_and)
+    ts(c3, p7, 3.0, A.is_lt)
+    ts(c4, p7, 4.0, A.is_lt)
+    scaled(col(ZQ, 15), blk, c3)
+    scaled(col(ZR, 15), blk, c4)
+    sel(col(SW, 0, 2), [[-2, 64]], A.not_equal, 1.0, -1)
+    sel(col(SW, 1, 2), [[-2, 64]], A.not_equal, 1.0, 0)
+    point(ZR, 15, 2, -1)
+    point(ZR, 15, 10, -1)
+    for o, x, c in ((HN, ID, -0.5), (IDK, ID, -512.0), (HP, ID, 0.5), (SWH, SW, -0.5), (WT, ID, c4)):
+        scaled(o, x, c)
+    for o, x in ((IDF, ID), (SWF, SW), (col(ZP, 14), blk)):
+        copy(o, x)
+    for c, row, v in ((4, 2, -64), (4, 10, -64), (5, 2, 64), (5, 10, 64), (5, 3, -64)):
+        point(WT, c, row, v)
+    point(WT, 1, 3, 32, 8)
+    for c, row, v in ((14, 4, 1), (14, 3, -16), (14, 2, 16), (14, 10, 16), (15, 5, 1), (15, 2, -16), (15, 10, -16)):
+        point(ZK2, c, row, v)
+    T1r, T1, T2 = new("bt", 128), new("bt", 128), [new("bt", 128), new("bt", 128)]
+    iota(T1r, [[0, 4], [256, 32]], 0, 0)
+    for h in (0, 1):
+        iota(T2[h], [[8192, 4], [0, 32]], 133120 + 32768 * h, 0)
+    rz = sub(RZ, 8, 136)
+    sel(rz, [[-16, 8], [-4, 8], [-1, 2]], A.not_equal, 1.0, 0)
+    sel(rz, [[-16, 8], [-4, 8], [0, 2]], A.not_equal, -1.0, -2)
+    sel(rz, [[0, 8], [-1, 2], [0, 8]], A.is_ge, 0.0, 0, 0)
+    ZG, WN = [[R("zz", z[1], z[2], 1, (0, 16)) for z in zs] for zs in ((ZG0, ZG1), (WN0, WN1))]
+    for h in (0, 1):
+        for c in (14, 15):
+            sel(col(ZG[h], c), [[-16, 9]], A.not_equal, 1.0, -8 * h, 8)
+        sel(col(WN[h], 7, 8), [[-16, 8], [0, 2]], A.not_equal, -1.0, -8 * h, 8)
+    sel(DM, [[-1, 128]], A.not_equal, 1.0, 0)
+    sel(col(DM, 0, 2), [[-2, 64]], A.not_equal, -1.0, -1)
+    sel(col(DM, 1, 2), [[-2, 64]], A.not_equal, -1.0, 0)
+    for a in range(4):
+        point(SZ, 12 + a, 4 * a + 2, 128)
+    ts(p4, pc0, 2, A.logical_shift_right, 3, A.bitwise_and)
+    ts(c01, p7, 2.0, A.is_lt, -32.0, A.mult)
+    ts(a64, p4, 64.0, A.mult)
+    scaled(col(ZK4, 14), blk, c01)
+    linear(T1, T1r, 1.0, a64)
+    tt(col(ZK4, 12), col(ZK4, 14), col(ZK2, 14), A.add)
+    tt(col(ZK4, 13), col(ZK4, 14), col(ZK2, 15), A.add)
+    ts(pa, pc0, 1, A.bitwise_and)
+    ts(tie, pa, 2048.0, A.mult)
+    fill(sub(gtab, 0, 16), 0.0)
+    fill(sub(gtab, 2064, 2080), 0.0)
 
-    L0, L1, L2 = new("bt", 128), new("bt", 128), new("bt", 128)
-    sw = [new("bt", 128) for t in range(3)]
-    a1, a2, b0, b1, b2 = [new("it", 128) for i in range(5)]
-    ts(a1, par, 2016, A.bitwise_and)
-    ts(a2, par, 31, A.bitwise_and)
-    ts(L0, par, 2048.0, A.is_ge, -2048.0, A.mult)
+    hi, lo, isp = new("bt", 128), new("bt", 128), new("bt", 128)
+    sw = [new("bt", 128), new("bt", 128), new("ft", 128)]
+    cp(hi, par)
     cp(sw[0], swi)
-    ts(L1, a1, 2.0, A.mult)
-    ts(L2, a2, 2.0, A.mult)
-    for q, ch, L in (("S", 0, L0), ("A", 3, sw[0]), ("S", 1, L1), ("A", 2, L2)):
-        for h in (0, 1):
-            dma(q, chan("tab0", ch, h), half(L, h))
-    dma("A", sub(WF, 2048, 4096), T.fa[:, 2048:4096])
-    dma("A", yb, T.ph[:])
-    gen8 = R("gen8", 0, 1024, 1, (0, 8))
-    dma("A", gen8, T.gen[:])
-    act(NSW, SW, F.Copy, -1.0)
-    for c in (14, 15):
-        act(col(ZB, c), col(ZC, 15), F.Copy, -1.0)
-        act(col(ZP, c), col(ZC, 15), F.Copy)
-    act(HP, ID, F.Copy, 0.5)
-    act(HN, ID, F.Copy, -0.5)
-
-    isp, isf, mT, f2, p1, p2, p3, p4, p5 = [new("bt", 128) for i in range(9)]
-    sp = [new("bt", 128) for t in range(3)]
-    ts(b0, par, -2048.0, A.add, 0.0, A.max)
-    ts(mT, par, 2048.0, A.is_ge, 64.0, A.mult)
-    ts(isf, par, 2048.0, A.is_lt)
-    ts(b1, b0, 7, A.bitwise_and)
-    ts(b2, b0, 3, A.logical_shift_right)
-    tt(sp[0], sw[0], mT, A.mult)
-    ts(p3, par, 2560.0, A.is_ge, 960.0, A.mult)
-    ts(p1, b1, 128.0, A.mult)
-    cp(p2, b2)
-    ts(half(p4, 0), half(isf, 0), ca, A.mult)
-    ts(half(p4, 1), half(isf, 1), cb, A.mult)
-    tt(p5, isf, chalf, A.mult)
-    fixed = (p1, p2, p3, p4, p5)
-    offT = new("ut", 128)
-    mmg(bank(2, 0, 128), [(ID, x) for x in (sp[0], p3, p1, p2, p4, p5)])
+    tt(lo, par, hi, A.subtract)
+    ts(isp, par, 2048.0, A.is_ge, -3072.0, A.mult)
     koff, kfin = new("ut", 256), new("ut", 256)
-    k3, k4, k5 = new("bt", 256), new("bt", 256), new("bt", 256)
-    k1, k2 = new("it", 256), new("it", 256)
-    pen = {1: new("bt", 128), 2: new("bt", 128)}
-    ts(k1, kd, 15, A.bitwise_and)
-    cp(offT, bank(2, 0, 128))
-    ts(k2, kd, 4, A.logical_shift_right, 127, A.bitwise_and)
-    ts(k5, kd, 5120.0, A.is_ge, 960.0, A.mult)
-    ts(k3, k1, 64.0, A.mult)
-    cp(k4, k2)
-    mmg(bank(4, 0, 256), [(ID, k5), (ID, k3), (ID, k4)])
-    ts(f2, isf, 2.0, A.mult)
-    ts(isp, mT, 1.0 / 64, A.mult)
-    ts(kcol, pi, -4096.0, A.mult, 4194320.0, A.add)
+    ts(koff, kd, -4080.0, A.add)
+    cp(genb, gen8)
+    act(sqt, genb, F.Square, 1.0, -2.0)
 
-    def penalties(fixed_rows):
-        genb = R("genb", 0, 1024, 1, (0, 8))
-        gi, odd = new("it", 128), new("it", 128)
+    def place(gr, b, ch, lst, stop=False):
+        mms(gr, [(sub(bank(b), a, 512, 8), slide(part(PK, a, 8), 7 - ch), lst) for a in range(8)], stop)
+
+    def table(e, h, b, keep):
+        linear(q4(tb, 2 * e + h), bank(b), sub(keep, e, e + 1), onec)
+
+    def column_static(gr):
+        mm(gr, bank(3, 0, 128), [(HN, hi), (HN, lo), (ID, isp)])
+
+    gr = [group(), group()]
+    for ch, lst in ((0, hi), (2, sw[0]), (1, lo)):
         for h in (0, 1):
-            cp(half(genb, h), half(gen8, h))
-            mmg(bank(2 + h, 0, 64), [(R("zz", ZG[1] + 14 - 2 * a, ZG[1] + 142 - 2 * a, 1, (0, 8)),
-                                      sub(half(genb, h), a, 512, 8)) for a in range(8)])
-            fixed_rows(h)
-        cp(half(gi, 0), bank(2, 0, 64))
-        ts(h1, pa, -0.5, A.mult, -4096.0, A.add)
-        ts(half(odd, 0), half(gi, 0), 1, A.bitwise_and)
-        cp(half(gi, 1), bank(3, 0, 64))
-        ts(half(pen[1], 0), half(odd, 0), 4096.0, A.mult, h1, A.add)
-        ts(half(odd, 1), half(gi, 1), 1, A.bitwise_and)
-        ts(h0, pa, -0.5, A.mult)
-        ts(half(pen[1], 1), half(odd, 1), 4096.0, A.mult, h1, A.add)
-        fill(m16, -16.0)
-        ts(pen[2], odd, -4096.0, A.mult, h0, A.add)
-
-    def to_list(z, src, h, swap=0):
-        return [(one(z, i ^ swap), sub(src, 1024 * h + i, 1024 * h + 1024, 16)) for i in range(16)]
-
-    def four(out, win, off, c, who="VAVA"):
-        gather(who[c], q4(out, c), win, q4(off, c))
-
-    def grandparents(G1, tb, offT, who="VAVA"):
+            place(gr[h], 2 + 2 * h, ch, half(lst, h), ch == 1)
+    offT = new("ut", 128)
+    go = group()
+    column_static(go)
+    mm(go, bank(3, 0, 128), [(IDK, sw[0])], True)
+    ts(offT, bank(3, 0, 128), -2.0, A.mult, -8176.0, A.add)
+    for e in (0, 1):
         for h in (0, 1):
-            four(G1, tb, offT, 2 * h, who)
-            four(G1, tb, offT, 2 * h + 1, who)
-            mmg(bank(6 + h, 0, 64), to_list(ZC, G1, h))
+            table(e, h, 2 + 2 * h, sc)
 
+    sel(col(PK, 3, 8), [[-2, 8], [-16, 9], [-17, 2]], A.not_equal, 1.0, 16)
+    ts(p3, pm, 3, A.bitwise_and)
+    ts(s1, p3, -1.0, A.mult, 3.0, A.add)
+    ts(s2, pm, 7.0, A.is_equal)
+    ts(s3, pm, 8.0, A.is_lt)
+    tt(s4, s1, s2, A.max)
+    ts(s1, s4, 2.0, A.min)
+    tt(sc2, s1, s3, A.mult)
+    ts(c7, p7, 7.0, A.is_equal, 8191.0, A.mult)
+    ts(c47, p7, 4.0, A.is_ge, c7, A.add)
+    scaled(col(ZA, 15), blk, c47)
+    for c, row in ((0, 0), (12, 0), (1, 1), (13, 1), (8, 8), (4, 8), (9, 9), (5, 9)):
+        point(WS, c, row, 0.5)
+    point(WS, 7, 3, 0.5, 8)
+    scaled(ID2, ID, 2.0)
+    scaled(NID, ID, -1.0)
+    for r, rows in ((0, (0, 8)), (1, (1, 9, 2, 10)), (2, (4, 12)), (3, (5, 13, 6, 14))):
+        for row in rows:
+            point(WG, 2 * r + 1, row, 1)
+    for r, v in ((1, 16), (3, 16), (4, -8192), (5, -8192), (6, -8192), (7, -8192)):
+        point(WG, 2 * r + 1, 3, v)
+    for r, row, v in ((4, 0, 1), (4, 8, 1), (5, 1, 1), (5, 9, 1), (5, 3, 16), (6, 2, 1), (6, 10, 1), (7, 2, -1), (7, 10, -1),
+                      (2, 3, -8192), (3, 3, -8192)):
+        point(WT2, 2 * r + 1, row, v)
+    for c in (0, 1):
+        iota(half(PN, c), [[0, 64], [16384, 2], [0, 4]], -8192, 0)
+    for c in range(8, 16):
+        iota(col(PN, c), [[0, 64]], (0, 0, -1, 1)[c // 2 - 4], 0)
+    for e in (0, 1):
+        sel(col(PN, e, 2), [[-2, 8], [-16, 8], [0, 8]], A.is_equal, 0.0, -e)
+    m16, par2 = new("bt", 64), new("ft", 2)
+    fill(m16, -16.0)
+    ts(sub(par2, 0, 1), pa, 0.0, A.is_equal)
+    ts(sub(par2, 1, 2), pa, 1.0, A.is_equal)
+    fill(sub(FIN, 0, 16), 4096.0)
+
+    def to_list(gr, out, z, src, h, swap=0):
+        for c in (0, 1):
+            mms(gr, [(out, one(z, i ^ swap), sub(half(src, h), i, 1024, 16)) for i in range(8 * c, 8 * c + 8)], c == 1)
+
+    def whole(gr, out, z, src, swap=0):
+        for c in (0, 1):
+            mms(gr, [(out, one(z, i ^ swap), sub(src, i, 2048, 16)) for i in range(8 * c, 8 * c + 8)], c == 1)
+
+    qf = new("ft", 128)
     others = [c for c in T.cores if c != core]
     far = [c for c in others if topo.die(c) != topo.die(core)]
     near = [c for c in others if topo.die(c) == topo.die(core)]
@@ -360,10 +442,10 @@ def rank_program(g, core, T, topo):
             e = topo.engines(core, c)
             mask[c] = (1 << e[4 * k + o]) | (1 << e[4 * k + 2 + o])
     per = 2 * len(others)
-    nsent = [0]
+    sends, landc = {}, R("land4", 0, 512)
 
     def send(land, s):
-        mine = sub(land, 64 * rank, 64 * rank + 64)
+        mine = part(land, rank, 8)
 
         def fn():
             tr = []
@@ -372,203 +454,198 @@ def rank_program(g, core, T, topo):
                 tr.append(RemoteDMATransfer(dst_ids=[DstId(rid=rid, pnc=pid)], dma_engine_mask=mask[c],
                                             remote_sem=T.sem[s], src=ap(mine), dst=ap(mine)))
             return g.remote_dma_fused(tr, local_sem=T.sem.sent)
-        nsent[0] += per
-        op("G", fn, [mine], [])
+        sends[s] = op({"G": fn}, [mine], [])
 
-    tb, landc = tab[0], R("landc", 0, 512)
+    pen = {1: new("bt", 128), 2: new("bt", 128)}
+    new("bt", 128)
+    tau0, dtau, tau = new("ft", 128), new("ft", 128), new("ft", 128)
+    ranks = [r for r in range(len(T.cores)) if r != rank]
+
     for t in (1, 2):
-        plan = PLAN[t]
-        nm = lambda s, w: R("%s_%d" % (s, t), 0, w)
-        G1, M1, M0, E1, E0 = [nm(s, 2048) for s in ("g1", "m1", "m0", "e1", "e0")]
-        MB, EB, KG = nm("mb", 1024), nm("eb", 1024), nm("kg", 4096)
-        land = [nm("landa", 512), nm("landb", 512)]
+        land = [R("land%d" % (2 * t - 2 + h), 0, 512) for h in (0, 1)]
         s = sw[t - 1]
         off2, off4, offa, offb = [new("ut", 128) for i in range(4)]
-        tc, nsw = new("bt", 128), new("bt", 128)
+        fptr = new("ft", 128)
+        mmg(bank(6, 0, 128), [(ID, hi), (ID, lo), (ID, isp), (HP, s)])
+        relu(fptr, bank(6, 0, 128), 2.0)
+        mmg(bank(7, 0, 128), [(SW, hi), (SW, lo), (SW, isp), (SWH, s)])
+        ts(offa, bank(7, 0, 128), 2.0, A.mult, 2049.0, A.add)
         if t == 1:
-            tt(tc, s, f2, A.mult)
-            cp(koff, bank(4, 0, 256))
-        mmg(bank(3, 0, 128), [(SW, L1), (SW, L2), (NSW, L0), (NSW, L0), (NSW, s)])
-        grandparents(G1, tb, offT, plan["g1"])
-        if t == 2:
-            tt(tc, s, f2, A.mult)
+            for h in (0, 1):
+                mmg(bank(7, 128 + 64 * h, 64), [(slide(ZG[h], 14 - 2 * a), sub(sqt, a, 512, 8)) for a in range(8)])
+            ts(pen[1], bank(7, 128, 128), 1.0, A.not_equal, -4096.0, A.mult)
+            linear(pen[2], pen[1], -1.0, -4096.0)
+        gather(G1, TB, offT, PLAN["g1"])
         for h in (0, 1):
-            cp(half(off2, h), bank(6 + h, 0, 64))
-            four(WB, WF, off2, 2 * h + 1)
-            ts(half(off4, h), bank(6 + h, 0, 64), 2048.0, A.add)
-            four(WB, WF, off2, 2 * h)
-        for h in (0, 1):
-            mmg(bank(2, 64 * h, 64), to_list(Z2, G1, h, 1) + [(SW, half(tc, h)), (SW, half(isp, h))])
+            gq = group()
+            mm(gq, bank(2 + 2 * h, 0, 64), [(IDF, half(fptr, h))])
+            to_list(gq, bank(2 + 2 * h, 0, 64), ZQ, G1, h)
+        gq = group()
+        mm(gq, bank(3, 0, 128), [(SWF, fptr)])
+        whole(gq, bank(3, 0, 128), ZR, G1, 1)
         if t == 1:
             mmg(bank(0), [(ID, half(yb, 0))])
             mmg(bank(1), [(ID, half(yb, 1))])
-        ts(offa, bank(3, 0, 128), 1.0, A.add)
-        ts(offb, bank(2, 0, 128), 2048.0, A.add)
-
-        def same(M, E, e, h):
-            tt(q4(E, 2 * e + h), sub(M, 1024 * h + e, 1024 * h + 1024, 2), half(Y, h), A.is_equal)
-
-        def base(h):
-            z = ZB if t == 1 else ZP
-            return [(ID, m16)] * (t - 1) + [(two(z, a), sub(half(EB, h), a, 512, 8)) for a in range(8)]
-
-        def count(E, h):
-            return [(one(ZC, 2 * a + 1 - e), sub(q4(E, 2 * e + h), a, 512, 8)) for e in (0, 1) for a in range(8)]
-
-        def valid_list(k):
-            mmg(bank(7, 64 * k, 64), [(ID, q4(x, k)) for x in (k3, k4, k5, iok, iok)]
-                + to_list(Z3, R("vg", 1024 * k, 1024 * k + 1024), 0))
-
-        def spread(h):
-            x0, x1 = new("bt", 64), new("bt", 64)
-            tt(x0, bank(6, 64 * h, 64), half(nsw, h), A.mult)
-            tt(x1, bank(6, 64 * h, 64), half(s, h), A.mult)
-            dma("S", chan("gtab", 0, h, 16), x0)
-            dma("S", chan("gtab", 1, h, 16), x1)
-
-        for c in range(4):
-            four(WC, WBF, off4, c)
-            mmg(bank(2 + c), [(ID, q4(WC, c))])
-            if c == 1 and t == 1:
-                dma("S", VC, half(WC, 0))
-        gather("A", half(M1, 1), WBF, half(offb, 1))
-        if t == 1:
-            for k in range(4):
-                gather("A", R("vg", 1024 * k, 1024 * k + 1024), tb, q4(koff, k))
-            gather("A", half(M0, 1), WFC, half(offa, 1))
-        else:
-            gather("A", q4(M1, 1), WBF, q4(offb, 1))
-        tt(q4(M1, 0), (WBF, q4(offb, 0)), q4(WC, 0), A.max)
-        tt(MB, sub(WC, 0, 2048, 2), sub(VP, 1, 2048, 2), A.max)
-        if t == 1:
-            tt(q4(M1, 1), (WBF, q4(offb, 1)), q4(WC, 1), A.max)
-            ts(nsw, s, -1.0, A.mult, 1.0, A.add)
-            tt(EB, MB, Y, A.is_equal)
-            mmg(bank(7, 256, 64), base(0))
-        else:
-            tt(half(M1, 1), half(M1, 1), half(VP, 1), A.max)
-            tt(q4(M1, 1), q4(M1, 1), q4(VP, 1), A.max)
-            ts(nsw, s, -1.0, A.mult, 1.0, A.add)
-            sg = new("bt", 1024)
-            for h in (0, 1):
-                mmg(bank(6 + h), [(HN, half(yb, h)), (HP, half(MB, h))])
-            for h in (0, 1):
-                act(half(sg, h), bank(6 + h), F.Sign)
-            for h in (0, 1):
-                act(half(EB, h), half(sg, h), F.Square)
-            gather("A", q4(M0, 0), WFC, q4(offa, 0))
-            gather("A", q4(M0, 1), WFC, q4(offa, 1))
-            gather("A", half(M0, 1), WFC, half(offa, 1))
-        same(M1, E1, 0, 0)
-        if t == 1:
-            cp(sub(landc, 64 * rank, 64 * rank + 64), bank(7, 256, 64))
-            send(landc, "arr4")
-        same(M1, E1, 1, 0)
-        mmg(bank(6, 0, 64), count(E1, 0) + base(0))
-        if t == 1:
-            valid_list(0)
-            valid_list(1)
-            tt(half(M1, 1), half(M1, 1), half(VP, 1), A.max)
-        same(M1, E1, 0, 1)
-        spread(0)
-        same(M1, E1, 1, 1)
-        mmg(bank(6, 64, 64), base(1) + count(E1, 1))
-        if t == 1:
-            valid_list(2)
-            valid_list(3)
-            tt(sub(M0, 0, 256), (WFC, sub(offa, 0, 16)), sub(VC, 0, 256), A.max)
-            spread(1)
-            tt(sub(M0, 256, 1024), (WFC, sub(offa, 16, 64)), sub(VC, 256, 1024), A.max)
-            ts(kfin, bank(7, 0, 256), kcol, A.add, 2064.0, A.min)
-        else:
-            tt(sub(M0, 0, 384), sub(M0, 0, 384), sub(VP, 0, 384), A.max)
-            spread(1)
-            tt(sub(M0, 384, 1024), sub(M0, 384, 1024), sub(VP, 384, 1024), A.max)
-        same(M0, E0, 0, 0)
-        same(M0, E0, 1, 0)
-        vote = [group(), group()]
-        mm(vote[0], bank(6, 0, 64), base(0) * (t - 1) + count(E0, 0))
-        tt(half(M0, 1), half(M0, 1), half(VP, 1), A.max)
-        same(M0, E0, 0, 1)
-        same(M0, E0, 1, 1)
-        mine = [sub(land[h], 64 * rank, 64 * rank + 64) for h in (0, 1)]
-        for n in range(8):
-            h, k = n // 4, n % 4
-            o = half(q4(KG, k), h)
-            gather(plan["kids"][n], o, gtab, half(q4(kfin, k), h))
-            mm(vote[h], bank(6 + h, 0, 64), [(two(ZK, a), sub(o, a, 512, 8)) for a in range(8)], k == 3)
-            if n == 1:
-                mm(vote[1], bank(7, 0, 64), base(1) + count(E0, 1))
-            if n == 4:
-                act(mine[0], bank(6, 0, 64), F.Copy)
-                send(land[0], "arr%d" % (2 * t - 2))
-        cp(mine[1], bank(7, 0, 64))
-        send(land[1], "arr%d" % (2 * t - 1))
-        z, fl = new("ft", 128), new("bt", 128)
-        offT = new("ut", 128)
-        ranks = [r for r in range(len(T.cores)) if r != rank]
-        old, tb = tb, tab[t]
-        tbk, gt = (6, 7, 2, 3), [group() for b in range(4)]
-        bz, bu, bo, go = bank(4, 0, 64), bank(5, 0, 64), bank(4, 128, 128), group()
-
-        def fixed_rows(b):
-            mm(gt[b], bank(tbk[b]), [(ID3, q4(old, b))])
-
-        def place(h, b):
-            for i in range(8 * b, 8 * b + 8):
-                mm(gt[2 * h + b], bank(tbk[2 * h + b], 64 * (i % 8), 64),
-                   [(sub(pick, 128 * i, 128 * i + 128), half(sw[t], h))], i % 8 == 7)
-
         for h in (0, 1):
-            slot = lambda r: sub(land[h], 64 * r, 64 * r + 64)
+            ts(half(off2, h), bank(2 + 2 * h, 0, 64), 4095.0, A.min)
+            cp(half(off4, h), bank(2 + 2 * h, 0, 64))
+            if t == 2:
+                copy(half(qf, h), bank(2 + 2 * h, 0, 64))
+        cp(offb, bank(3, 0, 128))
+        gather(WB, WF, off2, PLAN["wb"])
+        gather(WC, WFB, off4, PLAN["wc"])
+        vp = (2, 3, 4, 5)
+        for c in range(4):
+            if PLAN["m1"][t - 1][c] == "F" and (PLAN["m0"][t - 1][c] == "F" or c < 2):
+                mmg(bank(vp[c], 0, 256), [(ID, sub(q4(WC, c), 1, 512, 2))])
+                tt(q4(MB, c), sub(q4(WC, c), 0, 512, 2), bank(vp[c], 0, 256), A.max)
+            else:
+                mmg(bank(vp[c]), [(ID, q4(WC, c))])
+                tt(q4(MB, c), sub(q4(WC, c), 0, 512, 2), sub(bank(vp[c]), 1, 512, 2), A.max)
+            if PLAN["m0"][t - 1][c] == "F":
+                dma("S", q4(VC, c), q4(WC, c))
+        for h in (0, 1):
+            tt(half(EB, h), half(MB, h), half(Y, h), A.not_equal)
+        for c in range(4):
+            if PLAN["m1"][t - 1][c] == "F":
+                tt(q4(M1, c), (WFB, q4(offb, c)), q4(WC, c), A.max)
+            else:
+                gather(q4(M1, c), WFB, q4(offb, c), 1)
+                tt(q4(M1, c), q4(M1, c), bank(vp[c]), A.max)
+        if t == 1:
+            mmg(bank(6, 0, 64), [(two(ZP, a), sub(half(EB, 0), a, 512, 8)) for a in range(8)])
+            copy(part(landc, rank, 8), bank(6, 0, 64))
+            send(landc, "arr4")
+        n = PLAN["e1"]
+        for c in range(n):
+            for e in (0, 1):
+                tt(sub(part(E1, c, n), 1 - e, 2048 // n, 2), sub(part(M1, c, n), e, 2048 // n, 2), part(Y, c, n), A.is_equal)
+        for c, b in enumerate((6, 7, 2, 3)):
+            gg = group()
+            mms(gg, [(sub(bank(b), e, 512, 2), WT, q4(half(tb, e), c)) for e in (0, 1)])
+            mms(gg, [(sub(bank(b), e, 512, 2), two(ZP, 2), q4(EB, c)) for e in (0, 1)])
+            mm(gg, bank(b), [(two(ZP, 2), q4(E1, c))], True)
+            relu(q4(gt, c), bank(b), 1.0)
+
+        kl = koff if t == 1 else kfin
+        for c in range(4):
+            if PLAN["m0"][t - 1][c] == "F":
+                tt(q4(M0, c), (WCF, q4(offa, c)), q4(VC, c), A.max)
+            else:
+                gather(q4(M0, c), WCF, q4(offa, c), 1)
+                if c < 2:
+                    mmg(bank(vp[c]), [(ID, q4(WC, c))])
+                tt(q4(M0, c), q4(M0, c), bank(vp[c]), A.max)
+        xb = [2, 3]
+        for h in (0, 1):
+            vote, vb = group(), bank(6 + h, 0, 64)
+            if t == 2 or h == 1:
+                mm(vote, vb, [(two(ZP, a), sub(half(EB, h), a, 512, 8)) for a in range(8)])
+            for e in (0, 1):
+                tt(q4(E0, 2 * e + h), sub(half(M0, h), e, 1024, 2), half(Y, h), A.is_equal)
+                mm(vote, vb, [(one(ZC, 2 * a + 1 - e), sub(q4(E0, 2 * e + h), a, 512, 8)) for a in range(8)])
+            kg = [part(KG, 4 * h + k, 8) for k in range(4)]
+            for k in range(4):
+                gather(kg[k], gtab, part(kl, 2 * k + h, 8), 1)
+                if t == 2:
+                    mm(vote, vb, [(two(ZK2, a), sub(kg[k], a, 512, 8)) for a in range(8)], k == 3)
+            if t == 1:
+                for ks in PLAN["clamp"]:
+                    b = xb.pop(0)
+                    xb.append(b)
+                    gx = group()
+                    for j, k in enumerate(ks):
+                        mm(gx, bank(b, 128 * j, 128), [(ID, T1), (ID, T2[h])])
+                    for j, k in enumerate(ks):
+                        mm(gx, bank(b, 128 * j, 128), [(slide(ZK4, 12 - 4 * a), sub(kg[k], a, 512, 4)) for a in range(4)],
+                           j == len(ks) - 1)
+                    c = sub(half(CL, h), 128 * ks[0], 128 * ks[-1] + 128)
+                    ts(c, bank(b, 0, 128 * len(ks)), -32.0, A.max, 32.0, A.min)
+                    mm(vote, vb, [(slide(RZ, 8 - 8 * u), sub(part(c, j, len(ks)), u, 128, 2))
+                                  for j in range(len(ks)) for u in (0, 1)], ks[-1] == 3)
+            linear(part(land[h], rank, 8), vb, 1.0, -16.0)
+            send(land[h], "arr%d" % (2 * t - 2 + h))
+
+        gp = [group() for b in range(4)]
+        if t == 1:
+            kf = new("ft", 256)
+            gk = group()
+            for hh in (0, 1):
+                mms(gk, [(bank(5, 256 + 64 * k + 32 * hh, 32), slide(SZ, 12 - 4 * u), sub(part(CL, 4 * hh + k, 8), u, 128, 4))
+                         for k in range(4) for u in range(4)], hh == 1)
+            tt(kf, bank(5, 256, 256), kd, A.add)
+            ts(kfin, kf, -4080.0, A.add, 2064.0, A.min)
+            for n, o, a, b in ((0, bank(2), 0, 512), (1, bank(4, 0, 256), 512, 768), (2, bank(5, 0, 256), 768, 1024)):
+                mm(gp[n], o, [(WS, sub(tb, a, b)), (WS, sub(tb, 1024 + a, 1024 + b))])
+                mm(gp[n], o, [(WN[a // 512], sub(sqt, a % 512, a % 512 + b - a))])
+            go = group()
+            column_static(go)
+        else:
+            falt, pg, tc, td, tau1 = new("ft", 128), new("bt", 128), new("ft", 128), new("ft", 128), new("ft", 128)
+            mmg(bank(2, 0, 128), [(ID, hi), (ID, lo), (ID, isp), (HN, s)])
+            act(falt, bank(2, 0, 128), F.Relu, 2.0, 1.0)
+            gq = group()
+            mm(gq, bank(3, 384, 128), [(IDF, falt)])
+            whole(gq, bank(3, 384, 128), ZA, G1)
+            ts(pg, bank(3, 384, 128), 8192.0, A.is_ge, 8192.0, A.mult)
+            mmg(bank(3, 128, 128), [(IDF, qf), (ID, pg)])
+            mmg(bank(3, 0, 128), [(ID2, hi), (ID2, lo), (NID, pg), (ID, s)])
+            mmg(bank(3, 256, 128), [(ID2, hi), (ID2, lo), (NID, pg), (NID, s)])
+            linear(tc, bank(3, 0, 128), 1.0, 8192.0)
+            linear(td, bank(3, 256, 128), 1.0, 8193.0)
+            tt(tau0, bank(3, 128, 128), tc, A.min)
+            tt(tau1, bank(3, 384, 128), td, A.min)
+            tt(dtau, tau1, tau0, A.subtract)
+            lots = ((bank(4), 0, 512), (bank(5, 0, 256), 512, 768), (bank(2, 0, 256), 768, 1024))
+            for n, (o, a, b) in enumerate(lots):
+                for e in (0, 1):
+                    mm(gp[n], o, [(slide(WG, 1 - e), sub(G1, 2 * a + e, 2 * b, 2)),
+                                  (slide(WT2, 1 - e), sub(tb, 1024 * e + a, 1024 * e + b))])
+
+        z, fl, u = new("ft", 128), new("bt", 128), new("ft", 128)
+        offT = new("ut", 128)
+        for h in (0, 1):
+            bz, bu = bank(6, 256 + 64 * h, 64), bank(7, 256 + 64 * h, 64)
             gz, gu = group(), group()
-            more = [sub(landc, 64 * r, 64 * r + 64) for r in ranks + [rank]] if t == 1 and h == 0 else []
-            if t == 1 and h == 1:
-                fixed_rows(2)
-                fixed_rows(3)
-            mm(gz, bz, [(SW, x) for x in more + [slot(rank)]], pre=[("arr4", per)] if more else [])
-            mm(gu, bu, [(ID, x) for x in more + [slot(rank)]])
+            mm(gz, bz, [(DM, part(land[h], rank, 8))])
+            mm(gu, bu, [(ID, part(land[h], rank, 8)), (ID, half(pen[t], h))])
             if t == 1 and h == 0:
-                penalties(fixed_rows)
-            if t == 2 and h == 0:
-                for b in (2, 3, 0, 1):
-                    fixed_rows(b)
-            mm(gz, bz, [(SW, half(pen[t], h))])
-            mm(gu, bu, [(ID, half(pen[t], h))])
-            if h == 1:
-                place(0, 0)
-                place(0, 1)
-                act(q4(tb, 0), bank(tbk[0]), F.Copy)
-                cp(q4(tb, 1), bank(tbk[1]))
-            mm(gz, bz, [(SW, slot(r)) for r in ranks], True, pre=[("arr%d" % (2 * t - 2 + h), per)])
-            mm(gu, bu, [(ID, slot(r)) for r in ranks], True)
-            act(half(z, h), bz, F.Relu)
+                mm(gu, bu, [(ID, part(landc, r, 8)) for r in range(8)], pre=[("arr4", per)], after=[sends["arr4"]])
+            arr = "arr%d" % (2 * t - 2 + h)
+            for gv, bv, w in ((gz, bz, DM), (gu, bu, ID)):
+                mm(gv, bv, [(w, part(land[h], r, 8)) for r in ranks], True, pre=[(arr, per)], after=[sends[arr]])
+            act(half(z, h), bz, F.Relu, -4096.0, tie)
             tt(half(fl, h), bu, half(z, h), A.is_gt)
             tt(half(sw[t], h), half(s, h), half(fl, h), A.not_equal)
-            tt(half(sp[t], h), half(sw[t], h), half(mT, h), A.mult)
-        mm(go, bo, [(ID, x) for x in fixed])
-        place(1, 0)
-        mm(go, bo, [(ID, sp[t])], True)
-        place(1, 1)
-        act(q4(tb, 2), bank(tbk[2]), F.Copy)
-        cp(offT, bo)
-        cp(q4(tb, 3), bank(tbk[3]))
+            if t == 2:
+                for n in ((0,), (1, 2))[h]:
+                    o, a, b = lots[n]
+                    mms(gp[n], [(sub(o, i, b - a, 8), part(PN, i, 8), sub(fl, a // 8, b // 8)) for i in range(8)], True)
+                    for e in (0, 1):
+                        relu(sub(fin, 2 * a + e, 2 * b, 2), o, sub(par2, e, e + 1))
+                tt(half(u, h), half(fl, h), half(dtau, h), A.mult)
+                tt(half(tau, h), half(u, h), half(tau0, h), A.add)
+                ts(half(offT, h), half(tau, h), -4080.0, A.add)
+        if t == 1:
+            place(gp[0], 2, 2, half(sw[t], 0), True)
+            mm(go, bank(3, 0, 128), [(IDK, sw[t])], True)
+            for n, b in ((2, 5), (1, 4)):
+                mms(gp[n], [(sub(bank(b), a, 256, 8), slide(part(PK, a, 8), 5), q4(sw[t], n + 1)) for a in range(8)], True)
+            ts(offT, bank(3, 0, 128), -2.0, A.mult, -8176.0, A.add)
+            for e in (1, 0):
+                table(e, 0, 2, sc2)
+                for c, b in ((2, 4), (3, 5)):
+                    linear(part(tb, 4 * e + c, 8), bank(b, 0, 256), sub(sc2, e, e + 1), onec)
 
-    ysf, yaf, ff = new("ft", 128), new("ft", 128), new("ft", 128)
-    offg = new("ut", 128)
-    G1, G2 = R("g1f", 0, 2048), R("g2", 0, 2048)
-    grandparents(G1, tb, offT)
-    act(ysf, sw[2], F.Copy)
-    outs = [dma("S", T.ys[:], ysf)]
+    yaf = new("ft", 128)
+    outs = [dma("S", T.ys[:], sw[2])]
+    gather(M1, FIN, offT, PLAN["g1"])
     for h in (0, 1):
-        ts(half(offg, h), bank(6 + h, 0, 64), 2048.0, A.add, 2048.0, A.min)
-        four(G2, R("g1f", 0, 2064), offg, 2 * h + 1)
-        ts(half(ff, h), bank(6 + h, 0, 64), 0.0, A.max)
-        four(G2, R("g1f", 0, 2064), offg, 2 * h)
-        mmg(bank(2 + h, 0, 64), to_list(ZC, G2, h))
-    for h in (0, 1):
-        tt(half(yaf, h), bank(2 + h, 0, 64), half(ff, h), A.add)
+        gq = group()
+        mm(gq, bank(6 + h, 0, 64), [(ID, m16)])
+        to_list(gq, bank(6 + h, 0, 64), ZC, M1, h)
+        tt(half(yaf, h), bank(6 + h, 0, 64), half(tau, h), A.min)
         outs.append(dma("S", T.ya[:, 64 * h:64 * h + 64], half(yaf, h)))
-    op("S", None, [], [], after=outs)
-    op("G", None, [], [], pre=[("sent", nsent[0])])
-    emit(ops, Q, T)
+    op({"S": None}, [], [], hard=outs)
+    op({"G": None}, [], [], pre=[("sent", per * len(sends))], after=list(sends.values()))
+    emit(arrange(ops), Q, T)

from concourse.bass import DstId, RemoteDMATransfer
from concourse.mybir import AluOpType, ActivationFunctionType

BF, F32, I32, U16 = "bfloat16", "float32", "int32", "uint16"
ZW = 144
SCRATCH = {
    "parl": ("sbuf", [128, 128], I32), "swl": ("sbuf", [128, 128], I32), "kdl": ("sbuf", [128, 256], I32),
    "gen8": ("sbuf", [128, 1024], I32), "zz": ("sbuf", [128, 21 * ZW + 13 * 128], BF), "zf": ("sbuf", [128, 256], F32),
    "it": ("sbuf", [128, 512], I32), "ft": ("sbuf", [128, 4096], F32), "ut": ("sbuf", [128, 4096], U16),
    "ps": ("psum", [128, 4096], F32),
}
for _n, _w in (("genb", 1024), ("yb", 1024), ("win", 8192), ("gtab", 2080), ("tb", 2064), ("bt", 4096), ("g1", 2048),
               ("fin", 2064), ("pn", 2048), ("m1", 2048), ("m0", 2048), ("e1", 2048), ("e0", 2048), ("mb", 1024),
               ("eb", 1024), ("sg", 1024), ("vc", 2048), ("kg", 4096), ("cl", 1024),
               ("land0", 512), ("land1", 512), ("land2", 512), ("land3", 512), ("land4", 512)):
    SCRATCH[_n] = ("sbuf", [128, _w], BF)
NC, ND = 126, 16
SEMAPHORES = ["c%d" % i for i in range(NC)] + ["d%d" % i for i in range(ND)] + \
    ["arr0", "arr1", "arr2", "arr3", "arr4", "sent"]

PLAN = {"g1": 4, "wb": 4, "wc": 8, "m1": ("FFUU", "FFUU"), "m0": ("FFUU", "FFUU"), "e1": 4,
        "clamp": ((0, 1), (2,), (3,))}
ORDER = """6 8 0 1 2 7 3 13 4 5 32A 11 12 30A 31A 14 21 143 81 35A 141 23 15 88 34A 82 148 83 90 140 146 16 17 92 9 151 89 139 80 97A 70 144 22 91 18 79 84 142 10 93 19 99A 27 168 98V 26 94 169A 95 20 33A 100V 170 183 117 38 24A 25A 36A 37A 96 176V 177A 69 40 150 116 149 180 39 171 178V 179A 181 48 28 61 147 182 184 185 186 29 191 71 196A 73A 197V 187 66 52 44 57 58 41 51 145 193 188 190 189 192 199V 86 198A 49 42 112 67 200A 201V 202A 72 195 208 210 203A 194 62 209 74A 205A 204A 220 213 211 63 54 115 45 43 113 46 129 212 114 230 47 118 207A 206A 125 55 119 222A 221 216 245 214 60 87 172 218 226 173 249 217 215 232 123 120 255A 227A 224A 229 223 59 56 219 237 238 152 257A 174 234 239 231 153 241 225 242 240A 243 233 246 53 244A 236 247 235 250 248A 155 50 64 75 251 85 68 283 254 252A 267 273 268 265A 154 156 253 158 160 159 228 263A 76 259 274 264A 269 275 260 256 288A 261 292 293 270 271 314 266A 262 289V 277 272 294 290A 258 278 295 279 276 175V 280 104 308 296 281A 291A 109 105 282 157 284 126 302 298 299 161 286 122A 285 65 102 297 130 300 303 164 301 287 304 305 306V 307 131 127 312 319 167 77 103 106 107 78 165 309 124 101 110 111A 316 108 132 310 133 162 311 166 322 313 324 320 121A 321 323 134 137 328 327 329 138 325 326 128 330 331 136 334 332 163 317 333 315 342V 337 336 340A 339V 318 135 344A 335 345 343V 341A 347 338 346A 350V 349A 359 353 356 352V 351A 354 355 348 362 357 363 369A 370V 358 360 364A 365 366 371A 361 372V 407 367A 374V 373A 368 375A 383 381 393 411 376A 377A 386 384 382 385 378A 415 394 379A 387 380A 391 395A 389 419 399 412 400 408 425A 402 409 388 390 410A 401 396 413 397A 429 392 414A 404 420 403 416 426 417 444 418A 398 473 427A 459 405 406 424 421 460 474 422A 477 423 478 434A 461 462 436A 438V 435 463 440A 430 439 437 432 431 451A 428 433 441 453V 449A 452 447 454 442A 455A 443 450 445 448 464 446 456 465 457V 479 458 466 480 468V 481 470 492 482 483 467 484 485 493 486 469A 471 475 488A 472 494 524 489 495 490 496 476 487A 497 491 502 498 505 508 499 503A 506 518 513 500V 504A 501V 507 509A 510V 512A 511V 514 515 516 519 517 520 521 522 523"""


def overlap(a, b):
    if a[0] != b[0] or a[1] >= b[2] or b[1] >= a[2]:
        return False
    if a[3] > 1 and a[3] == b[3] and (a[1] - b[1]) % a[3]:
        return False
    return True


def banks(rs):
    s = set()
    for r in rs:
        if r[0] == "ps":
            s.update(range(r[1] // 512, (r[2] - 1) // 512 + 1))
    return s


def clash(e, o):
    return any(overlap(a, b) for a in e["w"] for b in o["r"] + o["w"]) or any(overlap(a, b) for a in e["r"] for b in o["w"])


def arrange(ops):
    words = ORDER.split() or [str(i) for i in range(len(ops))]
    order = [int(w.rstrip("VA")) for w in words]
    assert sorted(order) == list(range(len(ops)))
    for w, i in zip(words, order):
        ops[i]["q"] = w[-1] if w[-1] in "VA" else list(ops[i]["alt"])[0]
        ops[i]["hard"] = [order.index(m) for m in ops[i]["hard"]]
    return [ops[i] for i in order]


def emit(ops, Q, T):
    last = {}
    members = {}
    for n, o in enumerate(ops):
        o["bk"] = banks(o["r"] + o["w"])
        o["nm"] = set(r[0] for r in o["r"] + o["w"])
        if o["grp"] is not None:
            last[o["grp"]] = n
            members.setdefault(o["grp"], set()).add(n)
    known = {q: set() for q in Q}
    at = []
    waits = []
    for n, o in enumerate(ops):
        deps = set(o["hard"])
        k = known[o["q"]]
        for m in range(n):
            if m in k:
                continue
            e = ops[m]
            if e["alt"][e["q"]] is None or (e["grp"] is not None and e["grp"] == o["grp"]):
                continue
            if (e["q"] != o["q"] and e["bk"] & o["bk"]) or (e["nm"] & o["nm"] and clash(e, o)):
                deps.add(last[e["grp"]] if e["grp"] is not None and last[e["grp"]] < n else m)
        ws = []
        for m in sorted(deps, reverse=True):
            if m in k:
                continue
            ws.append(m)
            k.add(m)
            k |= at[m]
            if ops[m]["grp"] is not None and last[ops[m]["grp"]] == m:
                k |= members[ops[m]["grp"]]
        waits.append(ws)
        at.append(set(k))
    need = set(m for ws in waits for m in ws)
    pools = {True: [["d%d" % i, None, 0] for i in range(ND)], False: [["c%d" % i, None, 0] for i in range(NC)]}
    sig = {}
    for n, o in enumerate(ops):
        q = Q[o["q"]]
        for m in waits[n]:
            q.wait_ge(T.sem[sig[m][0]], sig[m][1])
        for s, v in o["pre"]:
            q.wait_ge(T.sem[s], v)
        fn = o["alt"][o["q"]]
        if fn is None:
            continue
        ins = fn()
        if n in need:
            pool = pools[o["dma"]]
            free = [s for s in pool if s[1] is None] or [s for s in pool if s[1] in at[n]]
            s = free[0]
            step = 16 if o["dma"] else 1
            s[1] = n
            s[2] += step
            ins.then_inc(T.sem[s[0]], step)
            sig[n] = (s[0], s[2])


def rank_program(g, core, T, topo):
    rank = T.rank_of(core)
    if rank is None:
        return
    A, F = AluOpType, ActivationFunctionType
    Q = {"G": g, "V": g.vector, "A": g.scalar, "P": g.tensor, "S": g.sync}
    ops = []
    used = {}
    ng = [0]

    def R(name, c0, c1, step=1, p=None):
        return (name, c0, c1, step, p)

    def sub(r, a, b, step=1):
        return (r[0], r[1] + a, r[1] + b, step, r[4])

    def part(r, k, n):
        w = (r[2] - r[1]) // n
        return sub(r, w * k, w * k + w)

    def half(r, h):
        return part(r, h, 2)

    def q4(r, c):
        return part(r, c, 4)

    def new(name, n):
        c = used.get(name, 0)
        used[name] = c + (n + 15) // 16 * 16
        return R(name, c, c + n)

    def ap(r):
        if len(r) == 2:
            return ap(r[0]).indirect(ap(r[1]))
        rows = slice(None) if r[4] is None else slice(*r[4])
        cols = slice(r[1], r[2]) if r[3] == 1 else slice(r[1], r[2], r[3])
        return T[r[0]][rows, cols]

    def regs(xs):
        out = []
        for x in xs:
            if isinstance(x, tuple):
                out += list(x) if len(x) == 2 else [x]
        return out

    def val(x):
        return ap(x) if isinstance(x, tuple) else x

    def op(alt, r, w, grp=None, first=False, last=False, dma=False, pre=(), after=(), hard=()):
        ops.append({"alt": alt, "r": regs(r), "w": regs(w), "grp": grp, "first": first, "last": last, "dma": dma,
                    "pre": list(pre), "after": list(after), "hard": list(hard)})
        return len(ops) - 1

    def dma(q, out, in_):
        return op({q: lambda: Q[q].dma_start(val(out), val(in_))}, [in_], [out], dma=True)

    def ts_(out, a, s1, o0, s2=None, o1=None):
        if o1 is None:
            return lambda: g.vector.tensor_scalar(ap(out), ap(a), val(s1), None, o0)
        return lambda: g.vector.tensor_scalar(ap(out), ap(a), val(s1), val(s2), o0, o1)

    def act_(out, a, f, scale=1.0, bias=0.0):
        kw = {n: x for n, x, plain in (("scale", scale, 1.0), ("bias", bias, 0.0)) if x != plain}
        return lambda: g.scalar.activation(ap(out), ap(a), f, **{n: val(x) for n, x in kw.items()})

    def ts(out, a, s1, o0, s2=None, o1=None):
        return op({"V": ts_(out, a, s1, o0, s2, o1)}, [a, s1, s2], [out])

    def tt(out, a, b, o):
        return op({"V": lambda: g.vector.tensor_tensor(ap(out), ap(a), ap(b), o)}, [a, b], [out])

    def cp_(out, a):
        return lambda: g.vector.tensor_copy(ap(out), ap(a))

    def cp(out, a):
        return op({"V": cp_(out, a)}, [a], [out])

    def fill(out, c):
        return op({"V": lambda: g.vector.memset(ap(out), c)}, [], [out])

    def act(out, a, f, scale=1.0, bias=0.0):
        return op({"A": act_(out, a, f, scale, bias)}, [a, scale, bias], [out])

    def either(v, a, r, w):
        return op({"V": v, "A": a}, r, w)

    def copy(out, a):
        return either(cp_(out, a), act_(out, a, F.Copy), [a], [out])

    def scaled(out, a, c):
        return either(ts_(out, a, c, A.mult), act_(out, a, F.Copy, c), [a, c], [out])

    def linear(out, a, s, b):
        return either(ts_(out, a, s, A.mult, b, A.add), act_(out, a, F.Identity, s, b), [a, s, b], [out])

    def relu(out, a, s):
        return either(ts_(out, a, s, A.mult, 0.0, A.max), act_(out, a, F.Relu, s), [a, s], [out])

    def gather(out, win, off, n):
        for c in range(n):
            copy(part(out, c, n), (win, part(off, c, n)))

    def sel(r, pattern, cmp, c, base, cm=1):
        return op({"G": lambda: g.affine_select(ap(r), ap(r), pattern, cmp, c, base, cm)}, [r], [r])

    def iota(r, pattern, base, cm):
        if r[0] == "it":
            return op({"G": lambda: g.iota(ap(r), pattern, base, cm)}, [], [r])
        return op({"G": lambda: g.iota(ap(r), pattern, base, cm, allow_small_or_imprecise_dtypes=True)}, [], [r])

    def group():
        ng[0] += 1
        return {"id": ng[0], "n": 0}

    def mms(gr, items, stop=False, pre=(), after=()):
        first = gr["n"] == 0
        gr["n"] += 1

        def fn():
            for i, (o, w, x) in enumerate(items):
                ins = g.tensor.matmul(ap(o), ap(w), ap(x), first and i == 0, stop and i == len(items) - 1)
            return ins
        return op({"P": fn}, [y for o, w, x in items for y in (w, x)], [o for o, w, x in items], grp=gr["id"],
                  first=first, last=stop, pre=pre, after=after)

    def mm(gr, out, pairs, stop=False, pre=(), after=()):
        return mms(gr, [(out, w, x) for w, x in pairs], stop, pre, after)

    def mmg(out, pairs):
        mm(group(), out, pairs, True)

    def bank(b, a=0, n=512):
        return R("ps", 512 * b + a, 512 * b + a + n)

    PK = new("zz", 8 * ZW)
    ID = new("zz", 128)
    ZC, ZP, ZQ, ZR = [new("zz", ZW) for i in range(4)]
    SW = new("zz", 128)
    ZK2, ZK4, RZ, SZ, ZG0, ZG1, ZA, WG, WT2 = [new("zz", ZW) for i in range(9)]
    WS, WN0, WN1, DM = [new("zz", 128) for i in range(4)]
    HP, HN, IDK, SWH, WT, ID2, NID = [new("zz", 128) for i in range(7)]
    IDF, SWF, PN = R("zf", 0, 128), R("zf", 128, 256), R("pn", 0, 1024)

    def slide(z, a):
        return sub(z, a, a + 128)

    def one(z, i):
        return slide(z, 15 - i)

    def two(z, a):
        return slide(z, 14 - 2 * a)

    def col(z, c, step=16):
        return sub(z, c, z[2] - z[1], step)

    def point(z, c, row, v, step=16):
        n = [[-16, (z[2] - z[1]) // 16]] + ([[0, 16 // step]] if step < 16 else [])
        sel(col(z, c, step), n, A.not_equal, float(v), -row)

    par, swi, kd = R("parl", 0, 128), R("swl", 0, 128), R("kdl", 0, 256)
    TB = R("tb", 0, 2064)
    tb = R("tb", 16, 2064)
    gtab, gt = R("gtab", 0, 2080), R("gtab", 16, 2064)
    G1, FIN, fin = R("g1", 0, 2048), R("fin", 0, 2064), R("fin", 16, 2064)
    WC, WF, WB = R("win", 0, 2048), R("win", 2048, 6144), R("win", 6144, 8192)
    WCF, WFB, VC = R("win", 0, 6144), R("win", 2048, 8192), R("vc", 0, 2048)
    yb, Y = R("yb", 0, 1024), R("ps", 0, 1024)
    M1, M0, E1, E0 = [R(n, 0, 2048) for n in ("m1", "m0", "e1", "e0")]
    MB, EB, KG, CL = R("mb", 0, 1024), R("eb", 0, 1024), R("kg", 0, 4096), R("cl", 0, 1024)
    gen8, genb, sqt = [R(n, 0, 512, 1, (0, 16)) for n in ("gen8", "genb", "sg")]

    dma("S", par, T.par[:])
    dma("A", swi, T.sw[:])
    for o, x in ((gen8, T.gen[:]), (WF, T.fa[:]), (yb, T.ph[:]), (kd, T.kd[:])):
        dma("S", o, x)
    pc, pm, p3, p7, pa, p4 = [new("it", 2) for i in range(3)] + [new("it", 1) for i in range(3)]
    sc0, sc, s1, s2, s3, s4, sc2 = [new("ft", 2) for i in range(7)]
    onec, c01, c3, c4, c7, c47, a64, tie = [new("ft", 1) for i in range(8)]
    pc0 = sub(pc, 0, 1)
    iota(pc, [[8, 2]], 0, 1)
    fill(PK, 0.0)
    fill(ID, 0.0)
    fill(R("zz", ZC[1], SW[2]), 0.0)
    fill(R("zz", ZK2[1], ZG1[2]), 0.0)
    fill(R("zz", ZA[1], DM[2]), 0.0)
    sel(col(PK, 7, 8), [[-2, 8], [-16, 9], [-1, 2]], A.not_equal, 1.0, 0)
    sel(ID, [[-1, 128]], A.not_equal, 1.0, 0)
    ts(pm, pc, 15, A.bitwise_and)
    ts(sc0, pm, -1.0, A.mult, 3.0, A.add)
    ts(sc, sc0, 0.0, A.max, 2.0, A.min)
    ts(onec, sub(pm, 0, 1), 3.0, A.is_equal)
    fill(sub(TB, 0, 16), 0.0)
    z2 = R("zz", ZC[1] + 15, ZP[2], 16)
    sel(z2, [[0, 2], [-16, 9]], A.is_ge, 1.0, -16)
    sel(z2, [[0, 2], [-16, 9]], A.is_ge, 0.0, 0)
    blk = col(ZC, 15)
    ts(p7, pc0, 7, A.bitwise_and)
    ts(c3, p7, 3.0, A.is_lt)
    ts(c4, p7, 4.0, A.is_lt)
    scaled(col(ZQ, 15), blk, c3)
    scaled(col(ZR, 15), blk, c4)
    sel(col(SW, 0, 2), [[-2, 64]], A.not_equal, 1.0, -1)
    sel(col(SW, 1, 2), [[-2, 64]], A.not_equal, 1.0, 0)
    point(ZR, 15, 2, -1)
    point(ZR, 15, 10, -1)
    for o, x, c in ((HN, ID, -0.5), (IDK, ID, -512.0), (HP, ID, 0.5), (SWH, SW, -0.5), (WT, ID, c4)):
        scaled(o, x, c)
    for o, x in ((IDF, ID), (SWF, SW), (col(ZP, 14), blk)):
        copy(o, x)
    for c, row, v in ((4, 2, -64), (4, 10, -64), (5, 2, 64), (5, 10, 64), (5, 3, -64)):
        point(WT, c, row, v)
    point(WT, 1, 3, 32, 8)
    for c, row, v in ((14, 4, 1), (14, 3, -16), (14, 2, 16), (14, 10, 16), (15, 5, 1), (15, 2, -16), (15, 10, -16)):
        point(ZK2, c, row, v)
    T1r, T1, T2 = new("bt", 128), new("bt", 128), [new("bt", 128), new("bt", 128)]
    iota(T1r, [[0, 4], [256, 32]], 0, 0)
    for h in (0, 1):
        iota(T2[h], [[8192, 4], [0, 32]], 133120 + 32768 * h, 0)
    rz = sub(RZ, 8, 136)
    sel(rz, [[-16, 8], [-4, 8], [-1, 2]], A.not_equal, 1.0, 0)
    sel(rz, [[-16, 8], [-4, 8], [0, 2]], A.not_equal, -1.0, -2)
    sel(rz, [[0, 8], [-1, 2], [0, 8]], A.is_ge, 0.0, 0, 0)
    ZG, WN = [[R("zz", z[1], z[2], 1, (0, 16)) for z in zs] for zs in ((ZG0, ZG1), (WN0, WN1))]
    for h in (0, 1):
        for c in (14, 15):
            sel(col(ZG[h], c), [[-16, 9]], A.not_equal, 1.0, -8 * h, 8)
        sel(col(WN[h], 7, 8), [[-16, 8], [0, 2]], A.not_equal, -1.0, -8 * h, 8)
    sel(DM, [[-1, 128]], A.not_equal, 1.0, 0)
    sel(col(DM, 0, 2), [[-2, 64]], A.not_equal, -1.0, -1)
    sel(col(DM, 1, 2), [[-2, 64]], A.not_equal, -1.0, 0)
    for a in range(4):
        point(SZ, 12 + a, 4 * a + 2, 128)
    ts(p4, pc0, 2, A.logical_shift_right, 3, A.bitwise_and)
    ts(c01, p7, 2.0, A.is_lt, -32.0, A.mult)
    ts(a64, p4, 64.0, A.mult)
    scaled(col(ZK4, 14), blk, c01)
    linear(T1, T1r, 1.0, a64)
    tt(col(ZK4, 12), col(ZK4, 14), col(ZK2, 14), A.add)
    tt(col(ZK4, 13), col(ZK4, 14), col(ZK2, 15), A.add)
    ts(pa, pc0, 1, A.bitwise_and)
    ts(tie, pa, 2048.0, A.mult)
    fill(sub(gtab, 0, 16), 0.0)
    fill(sub(gtab, 2064, 2080), 0.0)

    hi, lo, isp = new("bt", 128), new("bt", 128), new("bt", 128)
    sw = [new("bt", 128), new("bt", 128), new("ft", 128)]
    cp(hi, par)
    cp(sw[0], swi)
    tt(lo, par, hi, A.subtract)
    ts(isp, par, 2048.0, A.is_ge, -3072.0, A.mult)
    koff, kfin = new("ut", 256), new("ut", 256)
    ts(koff, kd, -4080.0, A.add)
    cp(genb, gen8)
    act(sqt, genb, F.Square, 1.0, -2.0)

    def place(gr, b, ch, lst, stop=False):
        mms(gr, [(sub(bank(b), a, 512, 8), slide(part(PK, a, 8), 7 - ch), lst) for a in range(8)], stop)

    def table(e, h, b, keep):
        linear(q4(tb, 2 * e + h), bank(b), sub(keep, e, e + 1), onec)

    def column_static(gr):
        mm(gr, bank(3, 0, 128), [(HN, hi), (HN, lo), (ID, isp)])

    gr = [group(), group()]
    for ch, lst in ((0, hi), (2, sw[0]), (1, lo)):
        for h in (0, 1):
            place(gr[h], 2 + 2 * h, ch, half(lst, h), ch == 1)
    offT = new("ut", 128)
    go = group()
    column_static(go)
    mm(go, bank(3, 0, 128), [(IDK, sw[0])], True)
    ts(offT, bank(3, 0, 128), -2.0, A.mult, -8176.0, A.add)
    for e in (0, 1):
        for h in (0, 1):
            table(e, h, 2 + 2 * h, sc)

    sel(col(PK, 3, 8), [[-2, 8], [-16, 9], [-17, 2]], A.not_equal, 1.0, 16)
    ts(p3, pm, 3, A.bitwise_and)
    ts(s1, p3, -1.0, A.mult, 3.0, A.add)
    ts(s2, pm, 7.0, A.is_equal)
    ts(s3, pm, 8.0, A.is_lt)
    tt(s4, s1, s2, A.max)
    ts(s1, s4, 2.0, A.min)
    tt(sc2, s1, s3, A.mult)
    ts(c7, p7, 7.0, A.is_equal, 8191.0, A.mult)
    ts(c47, p7, 4.0, A.is_ge, c7, A.add)
    scaled(col(ZA, 15), blk, c47)
    for c, row in ((0, 0), (12, 0), (1, 1), (13, 1), (8, 8), (4, 8), (9, 9), (5, 9)):
        point(WS, c, row, 0.5)
    point(WS, 7, 3, 0.5, 8)
    scaled(ID2, ID, 2.0)
    scaled(NID, ID, -1.0)
    for r, rows in ((0, (0, 8)), (1, (1, 9, 2, 10)), (2, (4, 12)), (3, (5, 13, 6, 14))):
        for row in rows:
            point(WG, 2 * r + 1, row, 1)
    for r, v in ((1, 16), (3, 16), (4, -8192), (5, -8192), (6, -8192), (7, -8192)):
        point(WG, 2 * r + 1, 3, v)
    for r, row, v in ((4, 0, 1), (4, 8, 1), (5, 1, 1), (5, 9, 1), (5, 3, 16), (6, 2, 1), (6, 10, 1), (7, 2, -1), (7, 10, -1),
                      (2, 3, -8192), (3, 3, -8192)):
        point(WT2, 2 * r + 1, row, v)
    for c in (0, 1):
        iota(half(PN, c), [[0, 64], [16384, 2], [0, 4]], -8192, 0)
    for c in range(8, 16):
        iota(col(PN, c), [[0, 64]], (0, 0, -1, 1)[c // 2 - 4], 0)
    for e in (0, 1):
        sel(col(PN, e, 2), [[-2, 8], [-16, 8], [0, 8]], A.is_equal, 0.0, -e)
    m16, par2 = new("bt", 64), new("ft", 2)
    fill(m16, -16.0)
    ts(sub(par2, 0, 1), pa, 0.0, A.is_equal)
    ts(sub(par2, 1, 2), pa, 1.0, A.is_equal)
    fill(sub(FIN, 0, 16), 4096.0)

    def to_list(gr, out, z, src, h, swap=0):
        for c in (0, 1):
            mms(gr, [(out, one(z, i ^ swap), sub(half(src, h), i, 1024, 16)) for i in range(8 * c, 8 * c + 8)], c == 1)

    def whole(gr, out, z, src, swap=0):
        for c in (0, 1):
            mms(gr, [(out, one(z, i ^ swap), sub(src, i, 2048, 16)) for i in range(8 * c, 8 * c + 8)], c == 1)

    qf = new("ft", 128)
    others = [c for c in T.cores if c != core]
    far = [c for c in others if topo.die(c) != topo.die(core)]
    near = [c for c in others if topo.die(c) == topo.die(core)]
    mask = {}
    for lot, o in ((far, 0), (near, 1)):
        for k, c in enumerate(lot):
            e = topo.engines(core, c)
            mask[c] = (1 << e[4 * k + o]) | (1 << e[4 * k + 2 + o])
    per = 2 * len(others)
    sends, landc = {}, R("land4", 0, 512)

    def send(land, s):
        mine = part(land, rank, 8)

        def fn():
            tr = []
            for c in others:
                rid, pid, se = topo.addr(c)
                tr.append(RemoteDMATransfer(dst_ids=[DstId(rid=rid, pnc=pid)], dma_engine_mask=mask[c],
                                            remote_sem=T.sem[s], src=ap(mine), dst=ap(mine)))
            return g.remote_dma_fused(tr, local_sem=T.sem.sent)
        sends[s] = op({"G": fn}, [mine], [])

    pen = {1: new("bt", 128), 2: new("bt", 128)}
    new("bt", 128)
    tau0, dtau, tau = new("ft", 128), new("ft", 128), new("ft", 128)
    ranks = [r for r in range(len(T.cores)) if r != rank]

    for t in (1, 2):
        land = [R("land%d" % (2 * t - 2 + h), 0, 512) for h in (0, 1)]
        s = sw[t - 1]
        off2, off4, offa, offb = [new("ut", 128) for i in range(4)]
        fptr = new("ft", 128)
        mmg(bank(6, 0, 128), [(ID, hi), (ID, lo), (ID, isp), (HP, s)])
        relu(fptr, bank(6, 0, 128), 2.0)
        mmg(bank(7, 0, 128), [(SW, hi), (SW, lo), (SW, isp), (SWH, s)])
        ts(offa, bank(7, 0, 128), 2.0, A.mult, 2049.0, A.add)
        if t == 1:
            for h in (0, 1):
                mmg(bank(7, 128 + 64 * h, 64), [(slide(ZG[h], 14 - 2 * a), sub(sqt, a, 512, 8)) for a in range(8)])
            ts(pen[1], bank(7, 128, 128), 1.0, A.not_equal, -4096.0, A.mult)
            linear(pen[2], pen[1], -1.0, -4096.0)
        gather(G1, TB, offT, PLAN["g1"])
        for h in (0, 1):
            gq = group()
            mm(gq, bank(2 + 2 * h, 0, 64), [(IDF, half(fptr, h))])
            to_list(gq, bank(2 + 2 * h, 0, 64), ZQ, G1, h)
        gq = group()
        mm(gq, bank(3, 0, 128), [(SWF, fptr)])
        whole(gq, bank(3, 0, 128), ZR, G1, 1)
        if t == 1:
            mmg(bank(0), [(ID, half(yb, 0))])
            mmg(bank(1), [(ID, half(yb, 1))])
        for h in (0, 1):
            ts(half(off2, h), bank(2 + 2 * h, 0, 64), 4095.0, A.min)
            cp(half(off4, h), bank(2 + 2 * h, 0, 64))
            if t == 2:
                copy(half(qf, h), bank(2 + 2 * h, 0, 64))
        cp(offb, bank(3, 0, 128))
        gather(WB, WF, off2, PLAN["wb"])
        gather(WC, WFB, off4, PLAN["wc"])
        vp = (2, 3, 4, 5)
        for c in range(4):
            if PLAN["m1"][t - 1][c] == "F" and (PLAN["m0"][t - 1][c] == "F" or c < 2):
                mmg(bank(vp[c], 0, 256), [(ID, sub(q4(WC, c), 1, 512, 2))])
                tt(q4(MB, c), sub(q4(WC, c), 0, 512, 2), bank(vp[c], 0, 256), A.max)
            else:
                mmg(bank(vp[c]), [(ID, q4(WC, c))])
                tt(q4(MB, c), sub(q4(WC, c), 0, 512, 2), sub(bank(vp[c]), 1, 512, 2), A.max)
            if PLAN["m0"][t - 1][c] == "F":
                dma("S", q4(VC, c), q4(WC, c))
        for h in (0, 1):
            tt(half(EB, h), half(MB, h), half(Y, h), A.not_equal)
        for c in range(4):
            if PLAN["m1"][t - 1][c] == "F":
                tt(q4(M1, c), (WFB, q4(offb, c)), q4(WC, c), A.max)
            else:
                gather(q4(M1, c), WFB, q4(offb, c), 1)
                tt(q4(M1, c), q4(M1, c), bank(vp[c]), A.max)
        if t == 1:
            mmg(bank(6, 0, 64), [(two(ZP, a), sub(half(EB, 0), a, 512, 8)) for a in range(8)])
            copy(part(landc, rank, 8), bank(6, 0, 64))
            send(landc, "arr4")
        n = PLAN["e1"]
        for c in range(n):
            for e in (0, 1):
                tt(sub(part(E1, c, n), 1 - e, 2048 // n, 2), sub(part(M1, c, n), e, 2048 // n, 2), part(Y, c, n), A.is_equal)
        for c, b in enumerate((6, 7, 2, 3)):
            gg = group()
            mms(gg, [(sub(bank(b), e, 512, 2), WT, q4(half(tb, e), c)) for e in (0, 1)])
            mms(gg, [(sub(bank(b), e, 512, 2), two(ZP, 2), q4(EB, c)) for e in (0, 1)])
            mm(gg, bank(b), [(two(ZP, 2), q4(E1, c))], True)
            relu(q4(gt, c), bank(b), 1.0)

        kl = koff if t == 1 else kfin
        for c in range(4):
            if PLAN["m0"][t - 1][c] == "F":
                tt(q4(M0, c), (WCF, q4(offa, c)), q4(VC, c), A.max)
            else:
                gather(q4(M0, c), WCF, q4(offa, c), 1)
                if c < 2:
                    mmg(bank(vp[c]), [(ID, q4(WC, c))])
                tt(q4(M0, c), q4(M0, c), bank(vp[c]), A.max)
        xb = [2, 3]
        for h in (0, 1):
            vote, vb = group(), bank(6 + h, 0, 64)
            if t == 2 or h == 1:
                mm(vote, vb, [(two(ZP, a), sub(half(EB, h), a, 512, 8)) for a in range(8)])
            for e in (0, 1):
                tt(q4(E0, 2 * e + h), sub(half(M0, h), e, 1024, 2), half(Y, h), A.is_equal)
                mm(vote, vb, [(one(ZC, 2 * a + 1 - e), sub(q4(E0, 2 * e + h), a, 512, 8)) for a in range(8)])
            kg = [part(KG, 4 * h + k, 8) for k in range(4)]
            for k in range(4):
                gather(kg[k], gtab, part(kl, 2 * k + h, 8), 1)
                if t == 2:
                    mm(vote, vb, [(two(ZK2, a), sub(kg[k], a, 512, 8)) for a in range(8)], k == 3)
            if t == 1:
                for ks in PLAN["clamp"]:
                    b = xb.pop(0)
                    xb.append(b)
                    gx = group()
                    for j, k in enumerate(ks):
                        mm(gx, bank(b, 128 * j, 128), [(ID, T1), (ID, T2[h])])
                    for j, k in enumerate(ks):
                        mm(gx, bank(b, 128 * j, 128), [(slide(ZK4, 12 - 4 * a), sub(kg[k], a, 512, 4)) for a in range(4)],
                           j == len(ks) - 1)
                    c = sub(half(CL, h), 128 * ks[0], 128 * ks[-1] + 128)
                    ts(c, bank(b, 0, 128 * len(ks)), -32.0, A.max, 32.0, A.min)
                    mm(vote, vb, [(slide(RZ, 8 - 8 * u), sub(part(c, j, len(ks)), u, 128, 2))
                                  for j in range(len(ks)) for u in (0, 1)], ks[-1] == 3)
            linear(part(land[h], rank, 8), vb, 1.0, -16.0)
            send(land[h], "arr%d" % (2 * t - 2 + h))

        gp = [group() for b in range(4)]
        if t == 1:
            kf = new("ft", 256)
            gk = group()
            for hh in (0, 1):
                mms(gk, [(bank(5, 256 + 64 * k + 32 * hh, 32), slide(SZ, 12 - 4 * u), sub(part(CL, 4 * hh + k, 8), u, 128, 4))
                         for k in range(4) for u in range(4)], hh == 1)
            tt(kf, bank(5, 256, 256), kd, A.add)
            ts(kfin, kf, -4080.0, A.add, 2064.0, A.min)
            for n, o, a, b in ((0, bank(2), 0, 512), (1, bank(4, 0, 256), 512, 768), (2, bank(5, 0, 256), 768, 1024)):
                mm(gp[n], o, [(WS, sub(tb, a, b)), (WS, sub(tb, 1024 + a, 1024 + b))])
                mm(gp[n], o, [(WN[a // 512], sub(sqt, a % 512, a % 512 + b - a))])
            go = group()
            column_static(go)
        else:
            falt, pg, tc, td, tau1 = new("ft", 128), new("bt", 128), new("ft", 128), new("ft", 128), new("ft", 128)
            mmg(bank(2, 0, 128), [(ID, hi), (ID, lo), (ID, isp), (HN, s)])
            act(falt, bank(2, 0, 128), F.Relu, 2.0, 1.0)
            gq = group()
            mm(gq, bank(3, 384, 128), [(IDF, falt)])
            whole(gq, bank(3, 384, 128), ZA, G1)
            ts(pg, bank(3, 384, 128), 8192.0, A.is_ge, 8192.0, A.mult)
            mmg(bank(3, 128, 128), [(IDF, qf), (ID, pg)])
            mmg(bank(3, 0, 128), [(ID2, hi), (ID2, lo), (NID, pg), (ID, s)])
            mmg(bank(3, 256, 128), [(ID2, hi), (ID2, lo), (NID, pg), (NID, s)])
            linear(tc, bank(3, 0, 128), 1.0, 8192.0)
            linear(td, bank(3, 256, 128), 1.0, 8193.0)
            tt(tau0, bank(3, 128, 128), tc, A.min)
            tt(tau1, bank(3, 384, 128), td, A.min)
            tt(dtau, tau1, tau0, A.subtract)
            lots = ((bank(4), 0, 512), (bank(5, 0, 256), 512, 768), (bank(2, 0, 256), 768, 1024))
            for n, (o, a, b) in enumerate(lots):
                for e in (0, 1):
                    mm(gp[n], o, [(slide(WG, 1 - e), sub(G1, 2 * a + e, 2 * b, 2)),
                                  (slide(WT2, 1 - e), sub(tb, 1024 * e + a, 1024 * e + b))])

        z, fl, u = new("ft", 128), new("bt", 128), new("ft", 128)
        offT = new("ut", 128)
        for h in (0, 1):
            bz, bu = bank(6, 256 + 64 * h, 64), bank(7, 256 + 64 * h, 64)
            gz, gu = group(), group()
            mm(gz, bz, [(DM, part(land[h], rank, 8))])
            mm(gu, bu, [(ID, part(land[h], rank, 8)), (ID, half(pen[t], h))])
            if t == 1 and h == 0:
                mm(gu, bu, [(ID, part(landc, r, 8)) for r in range(8)], pre=[("arr4", per)], after=[sends["arr4"]])
            arr = "arr%d" % (2 * t - 2 + h)
            for gv, bv, w in ((gz, bz, DM), (gu, bu, ID)):
                mm(gv, bv, [(w, part(land[h], r, 8)) for r in ranks], True, pre=[(arr, per)], after=[sends[arr]])
            act(half(z, h), bz, F.Relu, -4096.0, tie)
            tt(half(fl, h), bu, half(z, h), A.is_gt)
            tt(half(sw[t], h), half(s, h), half(fl, h), A.not_equal)
            if t == 2:
                for n in ((0,), (1, 2))[h]:
                    o, a, b = lots[n]
                    mms(gp[n], [(sub(o, i, b - a, 8), part(PN, i, 8), sub(fl, a // 8, b // 8)) for i in range(8)], True)
                    for e in (0, 1):
                        relu(sub(fin, 2 * a + e, 2 * b, 2), o, sub(par2, e, e + 1))
                tt(half(u, h), half(fl, h), half(dtau, h), A.mult)
                tt(half(tau, h), half(u, h), half(tau0, h), A.add)
                ts(half(offT, h), half(tau, h), -4080.0, A.add)
        if t == 1:
            place(gp[0], 2, 2, half(sw[t], 0), True)
            mm(go, bank(3, 0, 128), [(IDK, sw[t])], True)
            for n, b in ((2, 5), (1, 4)):
                mms(gp[n], [(sub(bank(b), a, 256, 8), slide(part(PK, a, 8), 5), q4(sw[t], n + 1)) for a in range(8)], True)
            ts(offT, bank(3, 0, 128), -2.0, A.mult, -8176.0, A.add)
            for e in (1, 0):
                table(e, 0, 2, sc2)
                for c, b in ((2, 4), (3, 5)):
                    linear(part(tb, 4 * e + c, 8), bank(b, 0, 256), sub(sc2, e, e + 1), onec)

    yaf = new("ft", 128)
    outs = [dma("S", T.ys[:], sw[2])]
    gather(M1, FIN, offT, PLAN["g1"])
    for h in (0, 1):
        gq = group()
        mm(gq, bank(6 + h, 0, 64), [(ID, m16)])
        to_list(gq, bank(6 + h, 0, 64), ZC, M1, h)
        tt(half(yaf, h), bank(6 + h, 0, 64), half(tau, h), A.min)
        outs.append(dma("S", T.ya[:, 64 * h:64 * h + 64], half(yaf, h)))
    op({"S": None}, [], [], hard=outs)
    op({"G": None}, [], [], pre=[("sent", per * len(sends))], after=list(sends.values()))
    emit(arrange(ops), Q, T)
